import numpy as np
import ml_dtypes


def mxq(x, axis, fmt="e4m3"):
    dtype, down = {"e4m3": (ml_dtypes.float8_e4m3fn, 7), "e5m2": (ml_dtypes.float8_e5m2, 14)}[fmt]
    v = np.moveaxis(np.asarray(x, np.float32).astype(ml_dtypes.bfloat16).astype(np.float64), axis, -1)
    blocks = v.reshape(v.shape[:-1] + (-1, 32))
    amax = np.abs(blocks).max(-1, keepdims=True)
    byte = np.maximum(np.where(amax > 0, np.frexp(amax)[1] - 1 + 127, 0) - down, 1)
    scale = np.exp2(byte - 127.0)
    codes = (blocks / scale).astype(np.float32).astype(dtype).astype(np.float64)
    return np.moveaxis((codes * scale).reshape(v.shape), -1, axis)


WIDE = False


def mx_kscale(k):
    if not WIDE:
        return np.ones(k)
    levels = np.array([10, -10, 5, -5, 0])
    if k % 512:
        return np.exp2(np.random.permutation(np.resize(levels, k // 32))).repeat(32)
    a = np.empty((k // 512, 16))
    for p in range(k // 512):
        a[p, :8] = np.random.permutation(np.resize(levels, 8))
        for g in range(8):
            far = levels[np.abs(levels - a[p, g]) >= 10]
            a[p, g + 8] = far[np.random.randint(len(far))]
    return np.exp2(a.ravel()).repeat(32)


def f64(x):
    return np.asarray(x).astype(np.float64)


def striped(idx):
    return np.tile(idx.reshape(-1, 16).T, (8, 1)).astype(np.uint16)


def unstriped(offs):
    return offs[:16].T.reshape(-1).astype(np.int64)


E2M1 = np.array([0.0, 0.5, 1.0, 1.5, 2.0, 3.0, 4.0, 6.0, -0.0, -0.5, -1.0, -1.5, -2.0, -3.0, -4.0, -6.0])


def pack_weight(w, fmt):
    k, n = w.shape
    w = f64(np.asarray(w, np.float32).astype(ml_dtypes.bfloat16)).reshape(k // 32, 32, n)
    amax = np.abs(w).max(1)
    if fmt == "e4m3":
        byte = np.frexp(amax)[1] - 1 + 127 - 7
    else:
        mant, ex = np.frexp(amax / 6.0)
        byte = np.where(mant > 0.5, ex, ex - 1) + 127
    byte = np.clip(np.where(amax > 0, byte, 1), 1, 254)
    scaled = (w * np.exp2(127.0 - byte)[:, None, :]).reshape(k, n).astype(np.float32)
    by_word = np.ascontiguousarray(scaled.reshape(k // 512, 128, 4, n).transpose(0, 1, 3, 2))
    if fmt == "e4m3":
        words = by_word.astype(ml_dtypes.float8_e4m3fn).view(np.uint8)
    else:
        c = by_word.astype(ml_dtypes.float4_e2m1fn).view(np.uint8) & 0xF
        words = (c[..., 0::2] | (c[..., 1::2] << 4)).reshape(k // 512, 128, 2 * n)
    return np.ascontiguousarray(words), np.ascontiguousarray(byte.astype(np.uint8).reshape(k // 512, 16, n))


def unpack_weight(words, scales, fmt):
    g, _, n = scales.shape
    words = np.ascontiguousarray(words).reshape(g, 128, n, -1)
    if fmt == "e4m3":
        vals = words.view(ml_dtypes.float8_e4m3fn).astype(np.float64)
    else:
        nib = np.empty((g, 128, n, 4), np.uint8)
        nib[..., 0::2] = words & 0xF
        nib[..., 1::2] = words >> 4
        vals = E2M1[nib]
    vals = vals * np.repeat(np.exp2(scales.astype(np.float64) - 127.0), 8, axis=1)[..., None]
    return vals.transpose(0, 1, 3, 2).reshape(g * 512, n)


def silu(v):
    return v / (1.0 + np.exp(-np.maximum(v, -700.0)))


K, T, E, C, H, N = 512, 768, 9, 256, 512, 128
TOP = 3


def by_expert(wq, xq):
    return np.concatenate([wq[e].T @ xq[:, e * C:(e + 1) * C] for e in range(E)], axis=1)


def setup_inputs():
    n = np.random.standard_normal
    s = mx_kscale(K)[:, None]
    u = mx_kscale(H)
    deal = np.repeat(np.arange(E), C).reshape(TOP, T)[:, np.random.permutation(T)]
    deal = np.take_along_axis(deal, np.argsort(np.random.rand(TOP, T), axis=0), axis=0)
    for _ in range(8):
        s_, t_ = np.random.permutation(T).reshape(2, -1); r = np.random.randint(TOP, size=T // 2); x, y = deal[r, s_].copy(), deal[r, t_].copy()
        ok = ~((deal[:, s_] == y).any(0) | (deal[:, t_] == x).any(0)); deal[r[ok], s_[ok]] = y[ok]; deal[r[ok], t_[ok]] = x[ok]
    order = np.lexsort((np.random.rand(TOP * T), deal.reshape(-1)))
    slot_token = order % T; pos = np.empty(TOP * T, np.int64); pos[order] = np.arange(TOP * T); pos = pos.reshape(TOP, T)
    g = np.random.uniform(0.5, 1.5, (TOP, T)); g = g / g.sum(0)
    w1 = [pack_weight(m, "e2m1") for m in n((E, K, H)) / np.sqrt(K) / s[None] * u[None, None, :]]
    w2 = [pack_weight(m, "e2m1") for m in n((E, H, N)) / np.sqrt(H) / u[None, :, None]]
    x = pack_weight(n((K, T)) * s, "e4m3")
    return {
        "x_words": x[0],
        "x_scales": x[1],
        "w1_words": np.stack([m[0] for m in w1]),
        "w1_scales": np.stack([m[1] for m in w1]),
        "w2_words": np.stack([m[0] for m in w2]),
        "w2_scales": np.stack([m[1] for m in w2]),
        "gate": np.stack([np.tile(r, (N, 1)) for r in g]).astype(np.float32),
        "offs": striped(slot_token),
        "pos1": striped(pos[0]),
        "pos2": striped(pos[1]),
        "pos3": striped(pos[2]),
    }


def reference(x_words, x_scales, w1_words, w1_scales, w2_words, w2_scales, gate, offs, pos1, pos2, pos3):
    idx = unstriped(offs)
    w1 = np.stack([unpack_weight(w1_words[e], w1_scales[e], "e2m1") for e in range(E)])
    w2 = np.stack([unpack_weight(w2_words[e], w2_scales[e], "e2m1") for e in range(E)])
    xq = unpack_weight(x_words, x_scales, "e4m3")[:, idx]
    h = silu(by_expert(w1, xq))
    y = by_expert(w2, mxq(h, 0, "e4m3"))
    return sum(f64(gate[r]) * y[:, unstriped(p)] for r, p in enumerate((pos1, pos2, pos3)))

@@ -1,0 +1,200 @@
+from contextlib import ExitStack
+
+import concourse.mybir as mybir
+from concourse.masks import make_identity
+
+K, T, E, C, H, N = 512, 768, 9, 256, 512, 128
+TOP = 3
+S = E * C
+FLOPS = 2 * S * (K * H + H * N)
+
+F32 = mybir.dt.float32
+BF16 = mybir.dt.bfloat16
+I32 = mybir.dt.int32
+U32 = mybir.dt.uint32
+U16 = mybir.dt.uint16
+U8 = mybir.dt.uint8
+FP8X4 = mybir.dt.float8_e4m3fn_x4
+FP4X4 = mybir.dt.float4_e2m1fn_x4
+SILU = mybir.ActivationFunctionType.Silu
+MULT = mybir.AluOpType.mult
+ADD = mybir.AluOpType.add
+
+P = 128
+CH = 128
+W1_GROUPS = ((0, 1), (1, 3), (3, 6), (6, 9))
+W1S_GROUPS = ((0, 2), (2, 9))
+COPY_ON_VECTOR = (6, 7, 8)
+EVAC_ON_VECTOR = (0, 1, 2, 3, 4)
+TOKEN_CUTS = (0, 320, 640, 768)
+
+
+def tile_moe_pkd_mlp_silu_kernel(
+    tc, x_words, x_scales, w1_words, w1_scales, w2_words, w2_scales, gate, offs, pos1, pos2, pos3, out
+):
+    nc = tc.nc
+    with ExitStack() as ctx:
+        lists = ctx.enter_context(tc.tile_pool(name="lists", bufs=1))
+        keep = ctx.enter_context(tc.tile_pool(name="keep", bufs=1))
+        work = ctx.enter_context(tc.tile_pool(name="work", bufs=4))
+        psum = ctx.enter_context(tc.psum_pool(name="psum", bufs=1))
+
+        offs_sb = lists.tile([P, S // 16], U16, name="offs_sb")
+        pos_sb = [lists.tile([P, T // 16], U16, name="pos_sb%d" % r) for r in range(TOP)]
+        xw = keep.tile([P, T], U32, name="xw", align_bytes=64)
+        xs = keep.tile([P, T], U8, name="xs", align_bytes=64)
+        w1w = [keep.tile([P, b - a, 2 * H], U8, name="w1w%d" % a, align_bytes=64) for a, b in W1_GROUPS]
+        w1s = [keep.tile([P, b - a, H], U8, name="w1s%d" % a, align_bytes=64) for a, b in W1S_GROUPS]
+        w2w = keep.tile([P, E, 2 * N], U8, name="w2w", align_bytes=64)
+        w2s = keep.tile([P, E, N], U8, name="w2s", align_bytes=64)
+        gate_sb = keep.tile([P, TOP, T], F32, name="gate_sb", align_bytes=64)
+        y = keep.tile([P, S], F32, name="y", align_bytes=64)
+        ident = keep.tile([P, P], F32, name="ident", align_bytes=64)
+        warm_in = keep.tile([P, 1], F32, name="warm_in")
+        warm_out = keep.tile([P, 1], F32, name="warm_out")
+
+        def load_scales(queue, plane, src):
+            for q in range(4):
+                queue.dma_start(
+                    plane[32 * q : 32 * q + 4].bitcast(I32),
+                    src[:, 4 * q : 4 * q + 4, :].rearrange("e r n -> r e n").bitcast(I32),
+                )
+
+        def load_w1_words(g, queue):
+            a, b = W1_GROUPS[g]
+            queue.dma_start(w1w[g][:].bitcast(I32), w1_words[a:b, 0].rearrange("e p n -> p e n").bitcast(I32))
+
+        nc.vector.memset(xs[:].bitcast(I32), 0)
+        nc.vector.memset(w1s[0][:].bitcast(I32), 0)
+        nc.vector.memset(warm_in[:], 0.0)
+        nc.vector.memset(w2s[:].bitcast(I32), 0)
+        nc.vector.memset(w1s[1][:].bitcast(I32), 0)
+        make_identity(nc, ident[:])
+
+        nc.sync.dma_start(xw[:].bitcast(I32), x_words[0].rearrange("p t r -> p (t r)").bitcast(I32))
+        for q, queue in enumerate((nc.scalar, nc.scalar, nc.sync, nc.sync)):
+            queue.dma_start(xs[32 * q : 32 * q + 4, :].bitcast(I32), x_scales[0, 4 * q : 4 * q + 4, :].bitcast(I32))
+        nc.sync.dma_start(offs_sb[:], offs)
+        load_w1_words(0, nc.scalar)
+        nc.scalar.activation(warm_out[:], warm_in[:], SILU)
+        load_scales(nc.sync, w1s[0], w1_scales[W1S_GROUPS[0][0] : W1S_GROUPS[0][1], 0])
+        load_w1_words(1, nc.sync)
+        load_scales(nc.sync, w1s[1], w1_scales[W1S_GROUPS[1][0] : W1S_GROUPS[1][1], 0])
+        load_scales(nc.sync, w2s, w2_scales[:, 0])
+        nc.sync.dma_start(w2w[:].bitcast(I32), w2_words[:, 0].rearrange("e p n -> p e n").bitcast(I32))
+        load_w1_words(2, nc.sync)
+        load_w1_words(3, nc.sync)
+        for r, pos in enumerate((pos1, pos2, pos3)):
+            nc.sync.dma_start(pos_sb[r][:], pos)
+        for r in range(TOP):
+            nc.sync.dma_start(gate_sb[:, r, :], gate[r])
+
+        def group_of(groups, tiles, e):
+            for g, (a, b) in enumerate(groups):
+                if a <= e < b:
+                    return tiles[g][:, e - a, :]
+
+        slot_words = {}
+        slot_scales = {}
+        hidden = {}
+        codes = {}
+        code_scales = {}
+
+        def gather_tokens(e):
+            pieces = ((0, CH), (CH, C)) if e == 0 else ((0, C),)
+            for a, b in pieces:
+                gw = work.tile([P, b - a], U32, name="gw", align_bytes=64)
+                gs = work.tile([P, b - a], U8, name="gs", align_bytes=64)
+                cols = offs_sb[:, (e * C + a) // 16 : (e * C + b) // 16]
+                nc.vector.tensor_copy(gw[:], xw[:].indirect(cols))
+                nc.vector.tensor_copy(gs[:], xs[:].indirect(cols))
+                for c in range(a // CH, b // CH):
+                    slot_words[e, c] = gw[:, c * CH - a : (c + 1) * CH - a]
+                    slot_scales[e, c] = gs[:, c * CH - a : (c + 1) * CH - a]
+
+        def first_layer(e):
+            for c in range(C // CH):
+                acc = psum.tile([P, H], F32, name="acc", bufs=4)
+                nc.tensor.matmul_mx(
+                    out=acc[:],
+                    lhsT=slot_words[e, c].bitcast(FP8X4),
+                    lhsT_scale=slot_scales[e, c],
+                    rhs=group_of(W1_GROUPS, w1w, e).bitcast(FP4X4),
+                    rhs_scale=group_of(W1S_GROUPS, w1s, e),
+                    start=True,
+                    stop=True,
+                )
+                h = work.tile([P, 2, P, 2], BF16, name="h", align_bytes=64, bufs=6)
+                nc.scalar.activation(h[:], acc[:].rearrange("s (p u d) -> s u p d", u=2, d=2), SILU)
+                hidden[e, c] = h
+
+        def turn_and_quantize(e):
+            turned = psum.tile([P, C // CH, 2, CH], F32, name="turned", bufs=2)
+            for c in range(C // CH):
+                pairs = hidden[e, c][:].rearrange("s u p d -> s (u p d)").bitcast(F32)
+                for u in range(2):
+                    nc.tensor.transpose(turned[:, c, u, :], pairs[:, u * P : (u + 1) * P], ident[:])
+            grouped = work.tile([P, C * 4], BF16, name="grouped", align_bytes=64)
+            dst = grouped[:].bitcast(F32).rearrange("p (c s u) -> p c s u", c=C // CH, u=2)
+            src = turned[:].rearrange("p c u s -> p c s u")
+            if e in COPY_ON_VECTOR:
+                nc.vector.tensor_copy(dst, src)
+            else:
+                nc.scalar.copy(dst, src)
+            codes[e] = work.tile([P, C], U32, name="hq", align_bytes=64)
+            code_scales[e] = work.tile([P, C], U8, name="hs", align_bytes=64)
+            nc.vector.quantize_mx(out=codes[e][:].bitcast(FP8X4), scales=code_scales[e][:], in_=grouped[:])
+
+        def second_layer(e):
+            res = psum.tile([P, C], F32, name="res", bufs=2)
+            nc.tensor.matmul_mx(
+                out=res[:],
+                lhsT=w2w[:, e, :].bitcast(FP4X4),
+                lhsT_scale=w2s[:, e, :],
+                rhs=codes[e][:].bitcast(FP8X4),
+                rhs_scale=code_scales[e][:],
+                start=True,
+                stop=True,
+            )
+            if e in EVAC_ON_VECTOR:
+                nc.vector.tensor_copy(y[:, e * C : (e + 1) * C], res[:])
+            else:
+                nc.scalar.copy(y[:, e * C : (e + 1) * C], res[:])
+
+        gather_tokens(0)
+        gather_tokens(1)
+        gather_tokens(2)
+        for step in range(E + 2):
+            if step < E:
+                first_layer(step)
+            if 1 <= step <= E:
+                turn_and_quantize(step - 1)
+            if step >= 2:
+                second_layer(step - 2)
+            if step + 3 < E:
+                gather_tokens(step + 3)
+
+        cuts = list(zip(TOKEN_CUTS[:-1], TOKEN_CUTS[1:]))
+        parts = [
+            [keep.tile([P, b - a], F32, name="part%d_%d" % (r, a), align_bytes=64) for r in range(TOP)] for a, b in cuts
+        ]
+
+        def fetch(j, r):
+            a, b = cuts[j]
+            nc.vector.tensor_tensor(
+                parts[j][r][:], y[:].indirect(pos_sb[r][:, a // 16 : b // 16]), gate_sb[:, r, a:b], MULT
+            )
+
+        def finish(j):
+            a, b = cuts[j]
+            nc.vector.tensor_tensor(parts[j][0][:], parts[j][0][:], parts[j][2][:], ADD)
+            nc.sync.dma_start(out[:, a:b], parts[j][0][:])
+
+        for j in range(len(cuts)):
+            fetch(j, 0)
+            if j > 0:
+                finish(j - 1)
+            fetch(j, 1)
+            fetch(j, 2)
+            nc.vector.tensor_tensor(parts[j][0][:], parts[j][0][:], parts[j][1][:], ADD)
+        finish(len(cuts) - 1)

@@ -22,10 +22,10 @@ ADD = mybir.AluOpType.add
 
 P = 128
 CH = 128
-W1_GROUPS = ((0, 1), (1, 3), (3, 6), (6, 9))
-W1S_GROUPS = ((0, 2), (2, 9))
-COPY_ON_VECTOR = (6, 7, 8)
-EVAC_ON_VECTOR = (0, 1, 2, 3, 4)
+W1_GROUPS = ((0, 2), (2, 5), (5, 7), (7, 9))
+W1S_GROUPS = ((0, 5), (5, 9))
+COPY_ON_VECTOR = (3, 5, 7)
+EVAC_ON_VECTOR = (1, 2, 3, 7, 8)
 TOKEN_CUTS = (0, 320, 640, 768)
 
 
@@ -53,8 +53,8 @@ def tile_moe_pkd_mlp_silu_kernel(
         warm_in = keep.tile([P, 1], F32, name="warm_in")
         warm_out = keep.tile([P, 1], F32, name="warm_out")
 
-        def load_scales(queue, plane, src):
-            for q in range(4):
+        def load_scales(queues, plane, src):
+            for q, queue in enumerate(queues):
                 queue.dma_start(
                     plane[32 * q : 32 * q + 4].bitcast(I32),
                     src[:, 4 * q : 4 * q + 4, :].rearrange("e r n -> r e n").bitcast(I32),
@@ -71,23 +71,23 @@ def tile_moe_pkd_mlp_silu_kernel(
         nc.vector.memset(w1s[1][:].bitcast(I32), 0)
         make_identity(nc, ident[:])
 
-        nc.sync.dma_start(xw[:].bitcast(I32), x_words[0].rearrange("p t r -> p (t r)").bitcast(I32))
-        for q, queue in enumerate((nc.scalar, nc.scalar, nc.sync, nc.sync)):
-            queue.dma_start(xs[32 * q : 32 * q + 4, :].bitcast(I32), x_scales[0, 4 * q : 4 * q + 4, :].bitcast(I32))
         nc.sync.dma_start(offs_sb[:], offs)
         load_w1_words(0, nc.scalar)
+        for q, queue in enumerate((nc.scalar, nc.scalar, nc.sync, nc.sync)):
+            queue.dma_start(xs[32 * q : 32 * q + 4, :].bitcast(I32), x_scales[0, 4 * q : 4 * q + 4, :].bitcast(I32))
+        nc.sync.dma_start(xw[:].bitcast(I32), x_words[0].rearrange("p t r -> p (t r)").bitcast(I32))
+        load_scales((nc.scalar, nc.scalar, nc.sync, nc.sync), w1s[0], w1_scales[W1S_GROUPS[0][0] : W1S_GROUPS[0][1], 0])
         nc.scalar.activation(warm_out[:], warm_in[:], SILU)
-        load_scales(nc.sync, w1s[0], w1_scales[W1S_GROUPS[0][0] : W1S_GROUPS[0][1], 0])
         load_w1_words(1, nc.sync)
-        load_scales(nc.sync, w1s[1], w1_scales[W1S_GROUPS[1][0] : W1S_GROUPS[1][1], 0])
-        load_scales(nc.sync, w2s, w2_scales[:, 0])
-        nc.sync.dma_start(w2w[:].bitcast(I32), w2_words[:, 0].rearrange("e p n -> p e n").bitcast(I32))
         load_w1_words(2, nc.sync)
+        load_scales((nc.sync,) * 4, w1s[1], w1_scales[W1S_GROUPS[1][0] : W1S_GROUPS[1][1], 0])
         load_w1_words(3, nc.sync)
-        for r, pos in enumerate((pos1, pos2, pos3)):
-            nc.sync.dma_start(pos_sb[r][:], pos)
+        load_scales((nc.sync,) * 4, w2s, w2_scales[:, 0])
         for r in range(TOP):
             nc.sync.dma_start(gate_sb[:, r, :], gate[r])
+        nc.sync.dma_start(w2w[:].bitcast(I32), w2_words[:, 0].rearrange("e p n -> p e n").bitcast(I32))
+        for r, pos in enumerate((pos1, pos2, pos3)):
+            nc.sync.dma_start(pos_sb[r][:], pos)
 
         def group_of(groups, tiles, e):
             for g, (a, b) in enumerate(groups):
@@ -103,8 +103,8 @@ def tile_moe_pkd_mlp_silu_kernel(
         def gather_tokens(e):
             pieces = ((0, CH), (CH, C)) if e == 0 else ((0, C),)
             for a, b in pieces:
-                gw = work.tile([P, b - a], U32, name="gw", align_bytes=64)
-                gs = work.tile([P, b - a], U8, name="gs", align_bytes=64)
+                gw = work.tile([P, b - a], U32, name="gw", align_bytes=64, bufs=5)
+                gs = work.tile([P, b - a], U8, name="gs", align_bytes=64, bufs=3)
                 cols = offs_sb[:, (e * C + a) // 16 : (e * C + b) // 16]
                 nc.vector.tensor_copy(gw[:], xw[:].indirect(cols))
                 nc.vector.tensor_copy(gs[:], xs[:].indirect(cols))
@@ -114,7 +114,7 @@ def tile_moe_pkd_mlp_silu_kernel(
 
         def first_layer(e):
             for c in range(C // CH):
-                acc = psum.tile([P, H], F32, name="acc", bufs=4)
+                acc = psum.tile([P, H], F32, name="acc", bufs=3)
                 nc.tensor.matmul_mx(
                     out=acc[:],
                     lhsT=slot_words[e, c].bitcast(FP8X4),
@@ -134,19 +134,19 @@ def tile_moe_pkd_mlp_silu_kernel(
                 pairs = hidden[e, c][:].rearrange("s u p d -> s (u p d)").bitcast(F32)
                 for u in range(2):
                     nc.tensor.transpose(turned[:, c, u, :], pairs[:, u * P : (u + 1) * P], ident[:])
-            grouped = work.tile([P, C * 4], BF16, name="grouped", align_bytes=64)
+            grouped = work.tile([P, C * 4], BF16, name="grouped", align_bytes=64, bufs=3)
             dst = grouped[:].bitcast(F32).rearrange("p (c s u) -> p c s u", c=C // CH, u=2)
             src = turned[:].rearrange("p c u s -> p c s u")
             if e in COPY_ON_VECTOR:
                 nc.vector.tensor_copy(dst, src)
             else:
                 nc.scalar.copy(dst, src)
-            codes[e] = work.tile([P, C], U32, name="hq", align_bytes=64)
-            code_scales[e] = work.tile([P, C], U8, name="hs", align_bytes=64)
+            codes[e] = work.tile([P, C], U32, name="hq", align_bytes=64, bufs=9)
+            code_scales[e] = work.tile([P, C], U8, name="hs", align_bytes=64, bufs=9)
             nc.vector.quantize_mx(out=codes[e][:].bitcast(FP8X4), scales=code_scales[e][:], in_=grouped[:])
 
         def second_layer(e):
-            res = psum.tile([P, C], F32, name="res", bufs=2)
+            res = psum.tile([P, C], F32, name="res", bufs=3)
             nc.tensor.matmul_mx(
                 out=res[:],
                 lhsT=w2w[:, e, :].bitcast(FP4X4),
@@ -163,16 +163,15 @@ def tile_moe_pkd_mlp_silu_kernel(
 
         gather_tokens(0)
         gather_tokens(1)
-        gather_tokens(2)
         for step in range(E + 2):
             if step < E:
                 first_layer(step)
+            if step + 2 < E:
+                gather_tokens(step + 2)
             if 1 <= step <= E:
                 turn_and_quantize(step - 1)
             if step >= 2:
                 second_layer(step - 2)
-            if step + 3 < E:
-                gather_tokens(step + 3)
 
         cuts = list(zip(TOKEN_CUTS[:-1], TOKEN_CUTS[1:]))
         parts = [

@@ -22,11 +22,18 @@ ADD = mybir.AluOpType.add
 
 P = 128
 CH = 128
-W1_GROUPS = ((0, 2), (2, 5), (5, 7), (7, 9))
-W1S_GROUPS = ((0, 5), (5, 9))
-COPY_ON_VECTOR = (3, 5, 7)
-EVAC_ON_VECTOR = (1, 2, 3, 7, 8)
-TOKEN_CUTS = (0, 320, 640, 768)
+W1_GROUPS = ((0, 2), (2, 5), (5, 8), (8, 9))
+W1S_GROUPS = ((0, 3), (3, 9))
+LOAD_ORDER = ("g1", "g2", "gate", "s1", "w2s", "g3", "w2w", "pos")
+DIRECT = (2, 4, 6, 7, 8)
+HALVES = (7, 8)
+COPY_ON_VECTOR = (5,)
+EVAC_ON_VECTOR = ((8, 1), 0, 3, 4, 5)
+PE_CUTS = (256, 256)
+VECTOR_CUTS = (160, 96)
+LOOK = 2
+GATHER_FIRST = False
+BUFS = {"acc": 4, "turned": 1, "res": 3, "h": 12, "grouped": 9, "hq": 9, "gw": 4, "gs": 3}
 
 
 def tile_moe_pkd_mlp_silu_kernel(
@@ -78,16 +85,21 @@ def tile_moe_pkd_mlp_silu_kernel(
         nc.sync.dma_start(xw[:].bitcast(I32), x_words[0].rearrange("p t r -> p (t r)").bitcast(I32))
         load_scales((nc.scalar, nc.scalar, nc.sync, nc.sync), w1s[0], w1_scales[W1S_GROUPS[0][0] : W1S_GROUPS[0][1], 0])
         nc.scalar.activation(warm_out[:], warm_in[:], SILU)
-        load_w1_words(1, nc.sync)
-        load_w1_words(2, nc.sync)
-        load_scales((nc.sync,) * 4, w1s[1], w1_scales[W1S_GROUPS[1][0] : W1S_GROUPS[1][1], 0])
-        load_w1_words(3, nc.sync)
-        load_scales((nc.sync,) * 4, w2s, w2_scales[:, 0])
-        for r in range(TOP):
-            nc.sync.dma_start(gate_sb[:, r, :], gate[r])
-        nc.sync.dma_start(w2w[:].bitcast(I32), w2_words[:, 0].rearrange("e p n -> p e n").bitcast(I32))
-        for r, pos in enumerate((pos1, pos2, pos3)):
-            nc.sync.dma_start(pos_sb[r][:], pos)
+        for what in LOAD_ORDER:
+            if what == "s1":
+                load_scales((nc.sync,) * 4, w1s[1], w1_scales[W1S_GROUPS[1][0] : W1S_GROUPS[1][1], 0])
+            elif what == "w2s":
+                load_scales((nc.sync,) * 4, w2s, w2_scales[:, 0])
+            elif what == "w2w":
+                nc.sync.dma_start(w2w[:].bitcast(I32), w2_words[:, 0].rearrange("e p n -> p e n").bitcast(I32))
+            elif what == "gate":
+                for r in range(TOP):
+                    nc.sync.dma_start(gate_sb[:, r, :], gate[r])
+            elif what == "pos":
+                for r, pos in enumerate((pos1, pos2, pos3)):
+                    nc.sync.dma_start(pos_sb[r][:], pos)
+            else:
+                load_w1_words(("g1", "g2", "g3").index(what) + 1, nc.sync)
 
         def group_of(groups, tiles, e):
             for g, (a, b) in enumerate(groups):
@@ -97,14 +109,32 @@ def tile_moe_pkd_mlp_silu_kernel(
         slot_words = {}
         slot_scales = {}
         hidden = {}
+        grouped = {}
         codes = {}
         code_scales = {}
+        dealt_words = {}
+        dealt_scales = {}
+
+        for e in DIRECT:
+            dealt_words[e] = keep.tile([P, 4, 2 * P], U8, name="dw%d" % e, align_bytes=64)
+            dealt_scales[e] = keep.tile([P, 4, P], U8, name="ds%d" % e, align_bytes=64)
+            nc.gpsimd.tensor_copy(
+                dealt_words[e][:].bitcast(U16),
+                group_of(W1_GROUPS, w1w, e).bitcast(U16).rearrange("p (m t) -> p t m", t=4),
+            )
+            nc.gpsimd.tensor_copy(dealt_scales[e][:], group_of(W1S_GROUPS, w1s, e).rearrange("p (m t) -> p t m", t=4))
+
+        def units(e):
+            return ((0, 1), (1, 2)) if e in HALVES else ((0, 2),)
+
+        def key(e, a):
+            return (e, a) if e in HALVES else e
 
         def gather_tokens(e):
             pieces = ((0, CH), (CH, C)) if e == 0 else ((0, C),)
             for a, b in pieces:
-                gw = work.tile([P, b - a], U32, name="gw", align_bytes=64, bufs=5)
-                gs = work.tile([P, b - a], U8, name="gs", align_bytes=64, bufs=3)
+                gw = work.tile([P, b - a], U32, name="gw", align_bytes=64, bufs=BUFS["gw"])
+                gs = work.tile([P, b - a], U8, name="gs", align_bytes=64, bufs=BUFS["gs"])
                 cols = offs_sb[:, (e * C + a) // 16 : (e * C + b) // 16]
                 nc.vector.tensor_copy(gw[:], xw[:].indirect(cols))
                 nc.vector.tensor_copy(gs[:], xs[:].indirect(cols))
@@ -113,87 +143,132 @@ def tile_moe_pkd_mlp_silu_kernel(
                     slot_scales[e, c] = gs[:, c * CH - a : (c + 1) * CH - a]
 
         def first_layer(e):
-            for c in range(C // CH):
-                acc = psum.tile([P, H], F32, name="acc", bufs=3)
+            for a, b in units(e):
+                if e in DIRECT:
+                    grouped[e, a] = work.tile([P, (b - a) * CH * 4], BF16, name="grouped", align_bytes=64, bufs=BUFS["grouped"])
+                for c in range(a, b):
+                    acc = psum.tile([P, H], F32, name="acc", bufs=BUFS["acc"])
+                    if e in DIRECT:
+                        for t in range(4):
+                            nc.tensor.matmul_mx(
+                                out=acc[:, t * CH : (t + 1) * CH],
+                                lhsT=dealt_words[e][:, t, :].bitcast(FP4X4),
+                                lhsT_scale=dealt_scales[e][:, t, :],
+                                rhs=slot_words[e, c].bitcast(FP8X4),
+                                rhs_scale=slot_scales[e, c],
+                                start=True,
+                                stop=True,
+                            )
+                        dst = grouped[e, a][:, (c - a) * 4 * CH : (c - a + 1) * 4 * CH].rearrange("p (s t) -> p s t", t=4)
+                        nc.scalar.activation(dst, acc[:].rearrange("p (t s) -> p s t", t=4), SILU)
+                    else:
+                        nc.tensor.matmul_mx(
+                            out=acc[:],
+                            lhsT=slot_words[e, c].bitcast(FP8X4),
+                            lhsT_scale=slot_scales[e, c],
+                            rhs=group_of(W1_GROUPS, w1w, e).bitcast(FP4X4),
+                            rhs_scale=group_of(W1S_GROUPS, w1s, e),
+                            start=True,
+                            stop=True,
+                        )
+                        h = work.tile([P, 2, P, 2], BF16, name="h", align_bytes=64, bufs=BUFS["h"])
+                        nc.scalar.activation(h[:], acc[:].rearrange("s (p u d) -> s u p d", u=2, d=2), SILU)
+                        hidden[e, c] = h
+
+        def turn_and_quantize(e):
+            for a, b in units(e):
+                if e not in DIRECT:
+                    turned = psum.tile([P, b - a, 2, CH], F32, name="turned", bufs=BUFS["turned"])
+                    for c in range(a, b):
+                        pairs = hidden[e, c][:].rearrange("s u p d -> s (u p d)").bitcast(F32)
+                        for u in range(2):
+                            nc.tensor.transpose(turned[:, c - a, u, :], pairs[:, u * P : (u + 1) * P], ident[:])
+                    grouped[e, a] = work.tile([P, (b - a) * CH * 4], BF16, name="grouped", align_bytes=64, bufs=BUFS["grouped"])
+                    dst = grouped[e, a][:].bitcast(F32).rearrange("p (c s u) -> p c s u", c=b - a, u=2)
+                    src = turned[:].rearrange("p c u s -> p c s u")
+                    if key(e, a) in COPY_ON_VECTOR:
+                        nc.vector.tensor_copy(dst, src)
+                    else:
+                        nc.scalar.copy(dst, src)
+                codes[e, a] = work.tile([P, (b - a) * CH], U32, name="hq", align_bytes=64, bufs=BUFS["hq"])
+                code_scales[e, a] = work.tile([P, (b - a) * CH], U8, name="hs", align_bytes=64, bufs=BUFS["hq"])
+                nc.vector.quantize_mx(out=codes[e, a][:].bitcast(FP8X4), scales=code_scales[e, a][:], in_=grouped[e, a][:])
+
+        def second_layer(e):
+            for a, b in units(e):
+                res = psum.tile([P, (b - a) * CH], F32, name="res", bufs=BUFS["res"])
                 nc.tensor.matmul_mx(
-                    out=acc[:],
-                    lhsT=slot_words[e, c].bitcast(FP8X4),
-                    lhsT_scale=slot_scales[e, c],
-                    rhs=group_of(W1_GROUPS, w1w, e).bitcast(FP4X4),
-                    rhs_scale=group_of(W1S_GROUPS, w1s, e),
+                    out=res[:],
+                    lhsT=w2w[:, e, :].bitcast(FP4X4),
+                    lhsT_scale=w2s[:, e, :],
+                    rhs=codes[e, a][:].bitcast(FP8X4),
+                    rhs_scale=code_scales[e, a][:],
                     start=True,
                     stop=True,
                 )
-                h = work.tile([P, 2, P, 2], BF16, name="h", align_bytes=64, bufs=6)
-                nc.scalar.activation(h[:], acc[:].rearrange("s (p u d) -> s u p d", u=2, d=2), SILU)
-                hidden[e, c] = h
+                dst = y[:, e * C + a * CH : e * C + b * CH]
+                if key(e, a) in EVAC_ON_VECTOR:
+                    nc.vector.tensor_copy(dst, res[:])
+                else:
+                    nc.scalar.copy(dst, res[:])
 
-        def turn_and_quantize(e):
-            turned = psum.tile([P, C // CH, 2, CH], F32, name="turned", bufs=2)
-            for c in range(C // CH):
-                pairs = hidden[e, c][:].rearrange("s u p d -> s (u p d)").bitcast(F32)
-                for u in range(2):
-                    nc.tensor.transpose(turned[:, c, u, :], pairs[:, u * P : (u + 1) * P], ident[:])
-            grouped = work.tile([P, C * 4], BF16, name="grouped", align_bytes=64, bufs=3)
-            dst = grouped[:].bitcast(F32).rearrange("p (c s u) -> p c s u", c=C // CH, u=2)
-            src = turned[:].rearrange("p c u s -> p c s u")
-            if e in COPY_ON_VECTOR:
-                nc.vector.tensor_copy(dst, src)
-            else:
-                nc.scalar.copy(dst, src)
-            codes[e] = work.tile([P, C], U32, name="hq", align_bytes=64, bufs=9)
-            code_scales[e] = work.tile([P, C], U8, name="hs", align_bytes=64, bufs=9)
-            nc.vector.quantize_mx(out=codes[e][:].bitcast(FP8X4), scales=code_scales[e][:], in_=grouped[:])
-
-        def second_layer(e):
-            res = psum.tile([P, C], F32, name="res", bufs=3)
-            nc.tensor.matmul_mx(
-                out=res[:],
-                lhsT=w2w[:, e, :].bitcast(FP4X4),
-                lhsT_scale=w2s[:, e, :],
-                rhs=codes[e][:].bitcast(FP8X4),
-                rhs_scale=code_scales[e][:],
-                start=True,
-                stop=True,
-            )
-            if e in EVAC_ON_VECTOR:
-                nc.vector.tensor_copy(y[:, e * C : (e + 1) * C], res[:])
-            else:
-                nc.scalar.copy(y[:, e * C : (e + 1) * C], res[:])
-
-        gather_tokens(0)
-        gather_tokens(1)
+        for e in range(LOOK):
+            gather_tokens(e)
         for step in range(E + 2):
             if step < E:
                 first_layer(step)
-            if step + 2 < E:
-                gather_tokens(step + 2)
+            if GATHER_FIRST and step + LOOK < E:
+                gather_tokens(step + LOOK)
             if 1 <= step <= E:
                 turn_and_quantize(step - 1)
             if step >= 2:
                 second_layer(step - 2)
+            if not GATHER_FIRST and step + LOOK < E:
+                gather_tokens(step + LOOK)
 
-        cuts = list(zip(TOKEN_CUTS[:-1], TOKEN_CUTS[1:]))
+        def fetch(part, r, a, b):
+            nc.vector.tensor_tensor(part[:], y[:].indirect(pos_sb[r][:, a // 16 : b // 16]), gate_sb[:, r, a:b], MULT)
+
+        a = 0
+        for width in PE_CUTS:
+            part = [keep.tile([P, width], F32, name="part%d_%d" % (r, a), align_bytes=64) for r in range(TOP)]
+            total = keep.tile([P, width], F32, name="total%d" % a, align_bytes=64)
+            for r in range(TOP):
+                fetch(part[r], r, a, a + width)
+            for blk in range(width // P):
+                cols = slice(blk * P, (blk + 1) * P)
+                tag = ("acc", "turned")[blk % 2]
+                summed = psum.tile([P, P], F32, name="summed", tag=tag, bufs=BUFS[tag])
+                for r in range(TOP):
+                    nc.tensor.matmul(
+                        summed[:], part[r][:, cols], ident[:], start=(r == 0), stop=(r == TOP - 1), is_transpose=True
+                    )
+                by_token = work.tile([P, P], F32, name="by_token", align_bytes=64)
+                nc.scalar.copy(by_token[:], summed[:])
+                back = psum.tile([P, P], F32, name="back", tag="res", bufs=BUFS["res"])
+                nc.tensor.transpose(back[:], by_token[:], ident[:])
+                nc.scalar.copy(total[:, cols], back[:])
+            nc.sync.dma_start(out[:, a : a + width], total[:])
+            a += width
+
+        cuts = []
+        for width in VECTOR_CUTS:
+            cuts.append((a, a + width))
+            a += width
         parts = [
             [keep.tile([P, b - a], F32, name="part%d_%d" % (r, a), align_bytes=64) for r in range(TOP)] for a, b in cuts
         ]
-
-        def fetch(j, r):
-            a, b = cuts[j]
-            nc.vector.tensor_tensor(
-                parts[j][r][:], y[:].indirect(pos_sb[r][:, a // 16 : b // 16]), gate_sb[:, r, a:b], MULT
-            )
 
         def finish(j):
             a, b = cuts[j]
             nc.vector.tensor_tensor(parts[j][0][:], parts[j][0][:], parts[j][2][:], ADD)
             nc.sync.dma_start(out[:, a:b], parts[j][0][:])
 
-        for j in range(len(cuts)):
-            fetch(j, 0)
+        for j, (a, b) in enumerate(cuts):
+            fetch(parts[j][0], 0, a, b)
             if j > 0:
                 finish(j - 1)
-            fetch(j, 1)
-            fetch(j, 2)
+            fetch(parts[j][1], 1, a, b)
+            fetch(parts[j][2], 2, a, b)
             nc.vector.tensor_tensor(parts[j][0][:], parts[j][0][:], parts[j][1][:], ADD)
         finish(len(cuts) - 1)

@@ -22,18 +22,16 @@ ADD = mybir.AluOpType.add
 
 P = 128
 CH = 128
-W1_GROUPS = ((0, 2), (2, 5), (5, 8), (8, 9))
-W1S_GROUPS = ((0, 3), (3, 9))
-LOAD_ORDER = ("g1", "g2", "gate", "s1", "w2s", "g3", "w2w", "pos")
-DIRECT = (2, 4, 6, 7, 8)
-HALVES = (7, 8)
-COPY_ON_VECTOR = (5,)
-EVAC_ON_VECTOR = ((8, 1), 0, 3, 4, 5)
-PE_CUTS = (256, 256)
-VECTOR_CUTS = (160, 96)
-LOOK = 2
-GATHER_FIRST = False
-BUFS = {"acc": 4, "turned": 1, "res": 3, "h": 12, "grouped": 9, "hq": 9, "gw": 4, "gs": 3}
+BANKS = 8
+STACKED = 8
+W1_GROUPS = ((0, 3), (3, 6), (6, 9))
+FIRST = 256
+EARLY = 768
+PAIRS = ((0, 2), (2, 4), (4, 6), (6, 8), (8, 9))
+EVAC_ON_VECTOR = (2, 3)
+LATE_CUTS = (768, 1280, 1664, 2048, 2304)
+SUMMED = ((0, 384), (384, 640))
+REST = 640
 
 
 def tile_moe_pkd_mlp_silu_kernel(
@@ -43,7 +41,6 @@ def tile_moe_pkd_mlp_silu_kernel(
     with ExitStack() as ctx:
         lists = ctx.enter_context(tc.tile_pool(name="lists", bufs=1))
         keep = ctx.enter_context(tc.tile_pool(name="keep", bufs=1))
-        work = ctx.enter_context(tc.tile_pool(name="work", bufs=4))
         psum = ctx.enter_context(tc.psum_pool(name="psum", bufs=1))
 
         offs_sb = lists.tile([P, S // 16], U16, name="offs_sb")
@@ -51,224 +48,179 @@ def tile_moe_pkd_mlp_silu_kernel(
         xw = keep.tile([P, T], U32, name="xw", align_bytes=64)
         xs = keep.tile([P, T], U8, name="xs", align_bytes=64)
         w1w = [keep.tile([P, b - a, 2 * H], U8, name="w1w%d" % a, align_bytes=64) for a, b in W1_GROUPS]
-        w1s = [keep.tile([P, b - a, H], U8, name="w1s%d" % a, align_bytes=64) for a, b in W1S_GROUPS]
+        s_raw = keep.tile([P, H], U8, name="s_raw", align_bytes=64)
+        s_dealt = keep.tile([P, 4, P], U8, name="s_dealt", align_bytes=64)
+        last_raw = keep.tile([P, H], U8, name="last_raw", align_bytes=64)
+        s_last = keep.tile([P, 4, P], U8, name="s_last", align_bytes=64)
+        s_planes = keep.tile([P, STACKED, 4, P], U8, name="s_planes", align_bytes=64)
         w2w = keep.tile([P, E, 2 * N], U8, name="w2w", align_bytes=64)
         w2s = keep.tile([P, E, N], U8, name="w2s", align_bytes=64)
         gate_sb = keep.tile([P, TOP, T], F32, name="gate_sb", align_bytes=64)
         y = keep.tile([P, S], F32, name="y", align_bytes=64)
         ident = keep.tile([P, P], F32, name="ident", align_bytes=64)
-        warm_in = keep.tile([P, 1], F32, name="warm_in")
-        warm_out = keep.tile([P, 1], F32, name="warm_out")
-
-        def load_scales(queues, plane, src):
-            for q, queue in enumerate(queues):
-                queue.dma_start(
-                    plane[32 * q : 32 * q + 4].bitcast(I32),
-                    src[:, 4 * q : 4 * q + 4, :].rearrange("e r n -> r e n").bitcast(I32),
-                )
+        zero = keep.tile([P, 1], F32, name="zero")
+        zero_bias = keep.tile([P, 1], F32, name="zero_bias")
+        dealt = [keep.tile([P, 4, 2 * P], U8, name="dealt%d" % e, align_bytes=64) for e in range(E)]
+        bank = [psum.tile([P, 4 * CH], F32, name="bank%d" % b) for b in range(BANKS)]
 
         def load_w1_words(g, queue):
             a, b = W1_GROUPS[g]
             queue.dma_start(w1w[g][:].bitcast(I32), w1_words[a:b, 0].rearrange("e p n -> p e n").bitcast(I32))
 
-        nc.vector.memset(xs[:].bitcast(I32), 0)
-        nc.vector.memset(w1s[0][:].bitcast(I32), 0)
-        nc.vector.memset(warm_in[:], 0.0)
+        def load_xs(q, queue):
+            queue.dma_start(xs[32 * q : 32 * q + 4, :].bitcast(I32), x_scales[0, 4 * q : 4 * q + 4, :].bitcast(I32))
+
+        def deal_words(e):
+            for g, (a, b) in enumerate(W1_GROUPS):
+                if a <= e < b:
+                    nc.gpsimd.tensor_copy(
+                        dealt[e][:].bitcast(U16), w1w[g][:, e - a, :].bitcast(U16).rearrange("p (m t) -> p t m", t=4)
+                    )
+
+        nc.gpsimd.memset(xs[:].bitcast(I32), 0)
+        nc.vector.memset(zero[:], 0.0)
+        nc.vector.memset(s_planes[:].rearrange("p j t m -> p (j t m)").bitcast(I32), 0)
         nc.vector.memset(w2s[:].bitcast(I32), 0)
-        nc.vector.memset(w1s[1][:].bitcast(I32), 0)
+        nc.vector.memset(last_raw[:].bitcast(I32), 0)
         make_identity(nc, ident[:])
 
+        nc.scalar.dma_start(s_raw[:].bitcast(I32), w1_scales[0:STACKED, 0].rearrange("e f n -> f e n").bitcast(I32))
         nc.sync.dma_start(offs_sb[:], offs)
-        load_w1_words(0, nc.scalar)
-        for q, queue in enumerate((nc.scalar, nc.scalar, nc.sync, nc.sync)):
-            queue.dma_start(xs[32 * q : 32 * q + 4, :].bitcast(I32), x_scales[0, 4 * q : 4 * q + 4, :].bitcast(I32))
+        load_xs(2, nc.scalar)
+        load_xs(0, nc.sync)
+        load_xs(3, nc.scalar)
+        load_xs(1, nc.sync)
         nc.sync.dma_start(xw[:].bitcast(I32), x_words[0].rearrange("p t r -> p (t r)").bitcast(I32))
-        load_scales((nc.scalar, nc.scalar, nc.sync, nc.sync), w1s[0], w1_scales[W1S_GROUPS[0][0] : W1S_GROUPS[0][1], 0])
-        nc.scalar.activation(warm_out[:], warm_in[:], SILU)
-        for what in LOAD_ORDER:
-            if what == "s1":
-                load_scales((nc.sync,) * 4, w1s[1], w1_scales[W1S_GROUPS[1][0] : W1S_GROUPS[1][1], 0])
-            elif what == "w2s":
-                load_scales((nc.sync,) * 4, w2s, w2_scales[:, 0])
-            elif what == "w2w":
-                nc.sync.dma_start(w2w[:].bitcast(I32), w2_words[:, 0].rearrange("e p n -> p e n").bitcast(I32))
-            elif what == "gate":
-                for r in range(TOP):
-                    nc.sync.dma_start(gate_sb[:, r, :], gate[r])
-            elif what == "pos":
-                for r, pos in enumerate((pos1, pos2, pos3)):
-                    nc.sync.dma_start(pos_sb[r][:], pos)
-            else:
-                load_w1_words(("g1", "g2", "g3").index(what) + 1, nc.sync)
+        load_w1_words(0, nc.sync)
+        nc.scalar.activation(zero_bias[:], zero[:], SILU)
 
-        def group_of(groups, tiles, e):
-            for g, (a, b) in enumerate(groups):
-                if a <= e < b:
-                    return tiles[g][:, e - a, :]
-
-        slot_words = {}
-        slot_scales = {}
-        hidden = {}
-        grouped = {}
-        codes = {}
-        code_scales = {}
-        dealt_words = {}
-        dealt_scales = {}
-
-        for e in DIRECT:
-            dealt_words[e] = keep.tile([P, 4, 2 * P], U8, name="dw%d" % e, align_bytes=64)
-            dealt_scales[e] = keep.tile([P, 4, P], U8, name="ds%d" % e, align_bytes=64)
-            nc.gpsimd.tensor_copy(
-                dealt_words[e][:].bitcast(U16),
-                group_of(W1_GROUPS, w1w, e).bitcast(U16).rearrange("p (m t) -> p t m", t=4),
+        nc.vector.tensor_copy(s_dealt[:], s_raw[:].rearrange("p (m t) -> p t m", t=4))
+        for q in range(4):
+            nc.sync.dma_start(
+                s_planes[32 * q : 32 * q + 4].rearrange("p j t m -> p j (t m)").bitcast(I32),
+                s_dealt[32 * q : 32 * q + 32].rearrange("p t m -> p (t m)").bitcast(I32),
             )
-            nc.gpsimd.tensor_copy(dealt_scales[e][:], group_of(W1S_GROUPS, w1s, e).rearrange("p (m t) -> p t m", t=4))
+        load_w1_words(1, nc.sync)
+        load_w1_words(2, nc.sync)
+        for q in range(4):
+            nc.sync.dma_start(last_raw[32 * q : 32 * q + 4, :].bitcast(I32), w1_scales[E - 1, 0, 4 * q : 4 * q + 4, :].bitcast(I32))
+        nc.sync.dma_start(w2w[:].bitcast(I32), w2_words[:, 0].rearrange("e p n -> p e n").bitcast(I32))
+        for q in range(4):
+            nc.sync.dma_start(
+                w2s[32 * q : 32 * q + 4].bitcast(I32),
+                w2_scales[:, 0, 4 * q : 4 * q + 4, :].rearrange("e r n -> r e n").bitcast(I32),
+            )
+        for r, pos in enumerate((pos1, pos2, pos3)):
+            nc.sync.dma_start(pos_sb[r][:], pos)
+        nc.sync.dma_start(gate_sb[:], gate.rearrange("r p t -> p r t"))
 
-        def units(e):
-            return ((0, 1), (1, 2)) if e in HALVES else ((0, 2),)
+        for e in range(E - 1):
+            deal_words(e)
+        nc.gpsimd.tensor_copy(s_last[:], last_raw[:].rearrange("p (m t) -> p t m", t=4))
+        deal_words(E - 1)
 
-        def key(e, a):
-            return (e, a) if e in HALVES else e
+        def w1_plane(e, t):
+            if e == E - 1:
+                return s_last[:, t, :]
+            return s_planes[:, e, t, :]
 
-        def gather_tokens(e):
-            pieces = ((0, CH), (CH, C)) if e == 0 else ((0, C),)
-            for a, b in pieces:
-                gw = work.tile([P, b - a], U32, name="gw", align_bytes=64, bufs=BUFS["gw"])
-                gs = work.tile([P, b - a], U8, name="gs", align_bytes=64, bufs=BUFS["gs"])
-                cols = offs_sb[:, (e * C + a) // 16 : (e * C + b) // 16]
-                nc.vector.tensor_copy(gw[:], xw[:].indirect(cols))
-                nc.vector.tensor_copy(gs[:], xs[:].indirect(cols))
-                for c in range(a // CH, b // CH):
-                    slot_words[e, c] = gw[:, c * CH - a : (c + 1) * CH - a]
-                    slot_scales[e, c] = gs[:, c * CH - a : (c + 1) * CH - a]
+        words_first = keep.tile([P, FIRST], U32, name="words_first", tag="held_words", align_bytes=64)
+        words_early = keep.tile([P, EARLY - FIRST], U32, name="words_early", align_bytes=64)
+        scales_first = keep.tile([P, FIRST], U8, name="scales_first", tag="held_scales", align_bytes=64)
+        scales_early = keep.tile([P, EARLY - FIRST], U8, name="scales_early", align_bytes=64)
 
-        def first_layer(e):
-            for a, b in units(e):
-                if e in DIRECT:
-                    grouped[e, a] = work.tile([P, (b - a) * CH * 4], BF16, name="grouped", align_bytes=64, bufs=BUFS["grouped"])
-                for c in range(a, b):
-                    acc = psum.tile([P, H], F32, name="acc", bufs=BUFS["acc"])
-                    if e in DIRECT:
-                        for t in range(4):
-                            nc.tensor.matmul_mx(
-                                out=acc[:, t * CH : (t + 1) * CH],
-                                lhsT=dealt_words[e][:, t, :].bitcast(FP4X4),
-                                lhsT_scale=dealt_scales[e][:, t, :],
-                                rhs=slot_words[e, c].bitcast(FP8X4),
-                                rhs_scale=slot_scales[e, c],
-                                start=True,
-                                stop=True,
-                            )
-                        dst = grouped[e, a][:, (c - a) * 4 * CH : (c - a + 1) * 4 * CH].rearrange("p (s t) -> p s t", t=4)
-                        nc.scalar.activation(dst, acc[:].rearrange("p (t s) -> p s t", t=4), SILU)
-                    else:
-                        nc.tensor.matmul_mx(
-                            out=acc[:],
-                            lhsT=slot_words[e, c].bitcast(FP8X4),
-                            lhsT_scale=slot_scales[e, c],
-                            rhs=group_of(W1_GROUPS, w1w, e).bitcast(FP4X4),
-                            rhs_scale=group_of(W1S_GROUPS, w1s, e),
-                            start=True,
-                            stop=True,
-                        )
-                        h = work.tile([P, 2, P, 2], BF16, name="h", align_bytes=64, bufs=BUFS["h"])
-                        nc.scalar.activation(h[:], acc[:].rearrange("s (p u d) -> s u p d", u=2, d=2), SILU)
-                        hidden[e, c] = h
+        def gather(dst, window, a, b):
+            nc.vector.tensor_copy(dst, window[:].indirect(offs_sb[:, a // 16 : b // 16]))
 
-        def turn_and_quantize(e):
-            for a, b in units(e):
-                if e not in DIRECT:
-                    turned = psum.tile([P, b - a, 2, CH], F32, name="turned", bufs=BUFS["turned"])
-                    for c in range(a, b):
-                        pairs = hidden[e, c][:].rearrange("s u p d -> s (u p d)").bitcast(F32)
-                        for u in range(2):
-                            nc.tensor.transpose(turned[:, c - a, u, :], pairs[:, u * P : (u + 1) * P], ident[:])
-                    grouped[e, a] = work.tile([P, (b - a) * CH * 4], BF16, name="grouped", align_bytes=64, bufs=BUFS["grouped"])
-                    dst = grouped[e, a][:].bitcast(F32).rearrange("p (c s u) -> p c s u", c=b - a, u=2)
-                    src = turned[:].rearrange("p c u s -> p c s u")
-                    if key(e, a) in COPY_ON_VECTOR:
-                        nc.vector.tensor_copy(dst, src)
-                    else:
-                        nc.scalar.copy(dst, src)
-                codes[e, a] = work.tile([P, (b - a) * CH], U32, name="hq", align_bytes=64, bufs=BUFS["hq"])
-                code_scales[e, a] = work.tile([P, (b - a) * CH], U8, name="hs", align_bytes=64, bufs=BUFS["hq"])
-                nc.vector.quantize_mx(out=codes[e, a][:].bitcast(FP8X4), scales=code_scales[e, a][:], in_=grouped[e, a][:])
+        grouped = [keep.tile([P, (b - a) * C * 4], BF16, name="grouped%d" % a, align_bytes=64) for a, b in PAIRS]
 
-        def second_layer(e):
-            for a, b in units(e):
-                res = psum.tile([P, (b - a) * CH], F32, name="res", bufs=BUFS["res"])
+        def first_layer(c, words, scales):
+            e = c // 2
+            acc = bank[c % BANKS]
+            for t in range(4):
                 nc.tensor.matmul_mx(
-                    out=res[:],
-                    lhsT=w2w[:, e, :].bitcast(FP4X4),
-                    lhsT_scale=w2s[:, e, :],
-                    rhs=codes[e, a][:].bitcast(FP8X4),
-                    rhs_scale=code_scales[e, a][:],
+                    out=acc[:, t * CH : (t + 1) * CH],
+                    lhsT=dealt[e][:, t, :].bitcast(FP4X4),
+                    lhsT_scale=w1_plane(e, t),
+                    rhs=words.bitcast(FP8X4),
+                    rhs_scale=scales,
                     start=True,
                     stop=True,
                 )
-                dst = y[:, e * C + a * CH : e * C + b * CH]
-                if key(e, a) in EVAC_ON_VECTOR:
-                    nc.vector.tensor_copy(dst, res[:])
-                else:
-                    nc.scalar.copy(dst, res[:])
+            dst = grouped[c // 4][:, (c % 4) * 4 * CH : (c % 4 + 1) * 4 * CH].rearrange("p (s t) -> p s t", t=4)
+            src = acc[:].rearrange("p (t s) -> p s t", t=4)
+            if c == 0:
+                nc.scalar.activation(dst, src, SILU, bias=zero_bias[:])
+            else:
+                nc.scalar.activation(dst, src, SILU)
 
-        for e in range(LOOK):
-            gather_tokens(e)
-        for step in range(E + 2):
-            if step < E:
-                first_layer(step)
-            if GATHER_FIRST and step + LOOK < E:
-                gather_tokens(step + LOOK)
-            if 1 <= step <= E:
-                turn_and_quantize(step - 1)
-            if step >= 2:
-                second_layer(step - 2)
-            if not GATHER_FIRST and step + LOOK < E:
-                gather_tokens(step + LOOK)
+        gather(scales_first[:], xs, 0, FIRST)
+        gather(scales_early[:], xs, FIRST, EARLY)
+        gather(words_first[:], xw, 0, FIRST)
+        gather(words_early[:], xw, FIRST, EARLY)
+        for c in range(FIRST // CH):
+            first_layer(c, words_first[:, c * CH : (c + 1) * CH], scales_first[:, c * CH : (c + 1) * CH])
+        words_late = keep.tile([P, S - EARLY], U32, name="words_late", tag="held_words", align_bytes=64)
+        scales_late = keep.tile([P, S - EARLY], U8, name="scales_late", tag="held_scales", align_bytes=64)
+        for a, b in zip(LATE_CUTS, LATE_CUTS[1:]):
+            gather(words_late[:, a - EARLY : b - EARLY], xw, a, b)
+            gather(scales_late[:, a - EARLY : b - EARLY], xs, a, b)
+        for c in range(FIRST // CH, 2 * E):
+            if c < EARLY // CH:
+                cols = slice(c * CH - FIRST, (c + 1) * CH - FIRST)
+                first_layer(c, words_early[:, cols], scales_early[:, cols])
+            else:
+                cols = slice((c - EARLY // CH) * CH, (c - EARLY // CH + 1) * CH)
+                first_layer(c, words_late[:, cols], scales_late[:, cols])
 
-        def fetch(part, r, a, b):
-            nc.vector.tensor_tensor(part[:], y[:].indirect(pos_sb[r][:, a // 16 : b // 16]), gate_sb[:, r, a:b], MULT)
+        codes = keep.tile([P, S], U32, name="codes", align_bytes=64)
+        code_scales = keep.tile([P, S], U8, name="code_scales", align_bytes=64)
+        for k, (a, b) in enumerate(PAIRS):
+            nc.vector.quantize_mx(
+                out=codes[:, a * C : b * C].bitcast(FP8X4), scales=code_scales[:, a * C : b * C], in_=grouped[k][:]
+            )
+        for k, (a, b) in enumerate(PAIRS):
+            res = bank[(2 * E - BANKS + k) % BANKS]
+            for e in range(a, b):
+                nc.tensor.matmul_mx(
+                    out=res[:, (e - a) * C : (e - a + 1) * C],
+                    lhsT=w2w[:, e, :].bitcast(FP4X4),
+                    lhsT_scale=w2s[:, e, :],
+                    rhs=codes[:, e * C : (e + 1) * C].bitcast(FP8X4),
+                    rhs_scale=code_scales[:, e * C : (e + 1) * C],
+                    start=True,
+                    stop=True,
+                )
+            if k in EVAC_ON_VECTOR:
+                nc.vector.tensor_copy(y[:, a * C : b * C], res[:, 0 : (b - a) * C])
+            else:
+                nc.scalar.copy(y[:, a * C : b * C], res[:, 0 : (b - a) * C])
 
-        a = 0
-        for width in PE_CUTS:
-            part = [keep.tile([P, width], F32, name="part%d_%d" % (r, a), align_bytes=64) for r in range(TOP)]
-            total = keep.tile([P, width], F32, name="total%d" % a, align_bytes=64)
+        part = [keep.tile([P, T], F32, name="part%d" % r, align_bytes=64) for r in range(TOP)]
+        by_token = keep.tile([P, REST], F32, name="by_token", align_bytes=64)
+        total = keep.tile([P, REST], F32, name="total", align_bytes=64)
+        for a, b in SUMMED + ((REST, T),):
             for r in range(TOP):
-                fetch(part[r], r, a, a + width)
-            for blk in range(width // P):
-                cols = slice(blk * P, (blk + 1) * P)
-                tag = ("acc", "turned")[blk % 2]
-                summed = psum.tile([P, P], F32, name="summed", tag=tag, bufs=BUFS[tag])
-                for r in range(TOP):
+                nc.vector.tensor_tensor(part[r][:, a:b], y[:].indirect(pos_sb[r][:, a // 16 : b // 16]), gate_sb[:, r, a:b], MULT)
+        nc.vector.tensor_tensor(part[0][:, REST:T], part[0][:, REST:T], part[1][:, REST:T], ADD)
+        nc.vector.tensor_tensor(part[0][:, REST:T], part[0][:, REST:T], part[2][:, REST:T], ADD)
+
+        for k, (a, b) in enumerate(SUMMED):
+            back = bank[REST // P + k]
+            for r in range(TOP):
+                for lo in range(a, b, P):
                     nc.tensor.matmul(
-                        summed[:], part[r][:, cols], ident[:], start=(r == 0), stop=(r == TOP - 1), is_transpose=True
+                        bank[lo // P][:, 0:P],
+                        part[r][:, lo : lo + P],
+                        ident[:],
+                        start=(r == 0),
+                        stop=(r == TOP - 1),
+                        is_transpose=True,
                     )
-                by_token = work.tile([P, P], F32, name="by_token", align_bytes=64)
-                nc.scalar.copy(by_token[:], summed[:])
-                back = psum.tile([P, P], F32, name="back", tag="res", bufs=BUFS["res"])
-                nc.tensor.transpose(back[:], by_token[:], ident[:])
-                nc.scalar.copy(total[:, cols], back[:])
-            nc.sync.dma_start(out[:, a : a + width], total[:])
-            a += width
-
-        cuts = []
-        for width in VECTOR_CUTS:
-            cuts.append((a, a + width))
-            a += width
-        parts = [
-            [keep.tile([P, b - a], F32, name="part%d_%d" % (r, a), align_bytes=64) for r in range(TOP)] for a, b in cuts
-        ]
-
-        def finish(j):
-            a, b = cuts[j]
-            nc.vector.tensor_tensor(parts[j][0][:], parts[j][0][:], parts[j][2][:], ADD)
-            nc.sync.dma_start(out[:, a:b], parts[j][0][:])
-
-        for j, (a, b) in enumerate(cuts):
-            fetch(parts[j][0], 0, a, b)
-            if j > 0:
-                finish(j - 1)
-            fetch(parts[j][1], 1, a, b)
-            fetch(parts[j][2], 2, a, b)
-            nc.vector.tensor_tensor(parts[j][0][:], parts[j][0][:], parts[j][1][:], ADD)
-        finish(len(cuts) - 1)
+            for lo in range(a, b, P):
+                nc.scalar.copy(by_token[:, lo : lo + P], bank[lo // P][:, 0:P])
+            for lo in range(a, b, P):
+                nc.tensor.transpose(back[:, lo - a : lo - a + P], by_token[:, lo : lo + P], ident[:])
+            nc.scalar.copy(total[:, a:b], back[:, 0 : b - a])
+            (nc.sync, nc.scalar)[k].dma_start(out[:, a:b], total[:, a:b])
+        nc.sync.dma_start(out[:, REST:T], part[0][:, REST:T])

@@ -25,11 +25,13 @@ CH = 128
 BANKS = 8
 STACKED = 8
 W1_GROUPS = ((0, 3), (3, 6), (6, 9))
-FIRST = 256
-EARLY = 768
+FIRST = 128
+EARLY = 640
 PAIRS = ((0, 2), (2, 4), (4, 6), (6, 8), (8, 9))
-EVAC_ON_VECTOR = (2, 3)
-LATE_CUTS = (768, 1280, 1664, 2048, 2304)
+QUANT = ((0, 4), (4, 6), (6, 8), (8, 9))
+EVAC_ON_VECTOR = (4,)
+DEALT_ON_VECTOR = (1, 2, 5, 8)
+LATE_CUTS = (640, 896, 1280, 1664, 2048, 2304)
 SUMMED = ((0, 384), (384, 640))
 REST = 640
 
@@ -73,7 +75,7 @@ def tile_moe_pkd_mlp_silu_kernel(
         def deal_words(e):
             for g, (a, b) in enumerate(W1_GROUPS):
                 if a <= e < b:
-                    nc.gpsimd.tensor_copy(
+                    (nc.vector if e in DEALT_ON_VECTOR else nc.gpsimd).tensor_copy(
                         dealt[e][:].bitcast(U16), w1w[g][:, e - a, :].bitcast(U16).rearrange("p (m t) -> p t m", t=4)
                     )
 
@@ -132,7 +134,7 @@ def tile_moe_pkd_mlp_silu_kernel(
         def gather(dst, window, a, b):
             nc.vector.tensor_copy(dst, window[:].indirect(offs_sb[:, a // 16 : b // 16]))
 
-        grouped = [keep.tile([P, (b - a) * C * 4], BF16, name="grouped%d" % a, align_bytes=64) for a, b in PAIRS]
+        grouped = keep.tile([P, S * 4], BF16, name="grouped", align_bytes=64)
 
         def first_layer(c, words, scales):
             e = c // 2
@@ -147,7 +149,7 @@ def tile_moe_pkd_mlp_silu_kernel(
                     start=True,
                     stop=True,
                 )
-            dst = grouped[c // 4][:, (c % 4) * 4 * CH : (c % 4 + 1) * 4 * CH].rearrange("p (s t) -> p s t", t=4)
+            dst = grouped[:, c * 4 * CH : (c + 1) * 4 * CH].rearrange("p (s t) -> p s t", t=4)
             src = acc[:].rearrange("p (t s) -> p s t", t=4)
             if c == 0:
                 nc.scalar.activation(dst, src, SILU, bias=zero_bias[:])
@@ -175,9 +177,11 @@ def tile_moe_pkd_mlp_silu_kernel(
 
         codes = keep.tile([P, S], U32, name="codes", align_bytes=64)
         code_scales = keep.tile([P, S], U8, name="code_scales", align_bytes=64)
-        for k, (a, b) in enumerate(PAIRS):
+        for a, b in QUANT:
             nc.vector.quantize_mx(
-                out=codes[:, a * C : b * C].bitcast(FP8X4), scales=code_scales[:, a * C : b * C], in_=grouped[k][:]
+                out=codes[:, a * C : b * C].bitcast(FP8X4),
+                scales=code_scales[:, a * C : b * C],
+                in_=grouped[:, 4 * a * C : 4 * b * C],
             )
         for k, (a, b) in enumerate(PAIRS):
             res = bank[(2 * E - BANKS + k) % BANKS]

@@ -27,11 +27,11 @@ STACKED = 8
 W1_GROUPS = ((0, 3), (3, 6), (6, 9))
 FIRST = 128
 EARLY = 640
-PAIRS = ((0, 2), (2, 4), (4, 6), (6, 8), (8, 9))
-QUANT = ((0, 4), (4, 6), (6, 8), (8, 9))
-EVAC_ON_VECTOR = (4,)
-DEALT_ON_VECTOR = (1, 2, 5, 8)
-LATE_CUTS = (640, 896, 1280, 1664, 2048, 2304)
+BANKFULS = ((0, 512), (512, 1024), (1024, 1536), (1536, 2048), (2048, 2176), (2176, 2304))
+QUANT = ((0, 1024), (1024, 1536), (1536, 2048), (2048, 2176), (2176, 2304))
+EVAC_ON_VECTOR = (2, 3)
+DEALT_ON_VECTOR = ()
+LATE_CUTS = (640, 1024, 1408, 1792, 2048, 2304)
 SUMMED = ((0, 384), (384, 640))
 REST = 640
 
@@ -41,6 +41,7 @@ def tile_moe_pkd_mlp_silu_kernel(
 ):
     nc = tc.nc
     with ExitStack() as ctx:
+        held = ctx.enter_context(tc.tile_pool(name="held", bufs=1))
         lists = ctx.enter_context(tc.tile_pool(name="lists", bufs=1))
         keep = ctx.enter_context(tc.tile_pool(name="keep", bufs=1))
         psum = ctx.enter_context(tc.psum_pool(name="psum", bufs=1))
@@ -51,7 +52,7 @@ def tile_moe_pkd_mlp_silu_kernel(
         xs = keep.tile([P, T], U8, name="xs", align_bytes=64)
         w1w = [keep.tile([P, b - a, 2 * H], U8, name="w1w%d" % a, align_bytes=64) for a, b in W1_GROUPS]
         s_raw = keep.tile([P, H], U8, name="s_raw", align_bytes=64)
-        s_dealt = keep.tile([P, 4, P], U8, name="s_dealt", align_bytes=64)
+        s_dealt = held.tile([P, 4, P], U8, name="s_dealt", align_bytes=64, offset=4 * (S - EARLY) - 256)
         last_raw = keep.tile([P, H], U8, name="last_raw", align_bytes=64)
         s_last = keep.tile([P, 4, P], U8, name="s_last", align_bytes=64)
         s_planes = keep.tile([P, STACKED, 4, P], U8, name="s_planes", align_bytes=64)
@@ -97,7 +98,7 @@ def tile_moe_pkd_mlp_silu_kernel(
         nc.scalar.activation(zero_bias[:], zero[:], SILU)
 
         nc.vector.tensor_copy(s_dealt[:], s_raw[:].rearrange("p (m t) -> p t m", t=4))
-        for q in range(4):
+        for q in (0, 2, 1, 3):
             nc.sync.dma_start(
                 s_planes[32 * q : 32 * q + 4].rearrange("p j t m -> p j (t m)").bitcast(I32),
                 s_dealt[32 * q : 32 * q + 32].rearrange("p t m -> p (t m)").bitcast(I32),
@@ -126,9 +127,9 @@ def tile_moe_pkd_mlp_silu_kernel(
                 return s_last[:, t, :]
             return s_planes[:, e, t, :]
 
-        words_first = keep.tile([P, FIRST], U32, name="words_first", tag="held_words", align_bytes=64)
+        words_first = keep.tile([P, FIRST], U32, name="words_first", align_bytes=64)
         words_early = keep.tile([P, EARLY - FIRST], U32, name="words_early", align_bytes=64)
-        scales_first = keep.tile([P, FIRST], U8, name="scales_first", tag="held_scales", align_bytes=64)
+        scales_first = keep.tile([P, FIRST], U8, name="scales_first", align_bytes=64)
         scales_early = keep.tile([P, EARLY - FIRST], U8, name="scales_early", align_bytes=64)
 
         def gather(dst, window, a, b):
@@ -162,8 +163,8 @@ def tile_moe_pkd_mlp_silu_kernel(
         gather(words_early[:], xw, FIRST, EARLY)
         for c in range(FIRST // CH):
             first_layer(c, words_first[:, c * CH : (c + 1) * CH], scales_first[:, c * CH : (c + 1) * CH])
-        words_late = keep.tile([P, S - EARLY], U32, name="words_late", tag="held_words", align_bytes=64)
-        scales_late = keep.tile([P, S - EARLY], U8, name="scales_late", tag="held_scales", align_bytes=64)
+        words_late = held.tile([P, S - EARLY], U32, name="words_late", align_bytes=64, offset=0)
+        scales_late = held.tile([P, S - EARLY], U8, name="scales_late", align_bytes=64, offset=4 * (S - EARLY))
         for a, b in zip(LATE_CUTS, LATE_CUTS[1:]):
             gather(words_late[:, a - EARLY : b - EARLY], xw, a, b)
             gather(scales_late[:, a - EARLY : b - EARLY], xs, a, b)
@@ -178,27 +179,24 @@ def tile_moe_pkd_mlp_silu_kernel(
         codes = keep.tile([P, S], U32, name="codes", align_bytes=64)
         code_scales = keep.tile([P, S], U8, name="code_scales", align_bytes=64)
         for a, b in QUANT:
-            nc.vector.quantize_mx(
-                out=codes[:, a * C : b * C].bitcast(FP8X4),
-                scales=code_scales[:, a * C : b * C],
-                in_=grouped[:, 4 * a * C : 4 * b * C],
-            )
-        for k, (a, b) in enumerate(PAIRS):
+            nc.vector.quantize_mx(out=codes[:, a:b].bitcast(FP8X4), scales=code_scales[:, a:b], in_=grouped[:, 4 * a : 4 * b])
+        for k, (a, b) in enumerate(BANKFULS):
             res = bank[(2 * E - BANKS + k) % BANKS]
-            for e in range(a, b):
+            for lo in range(a, b, C):
+                hi = min(b, lo + C)
                 nc.tensor.matmul_mx(
-                    out=res[:, (e - a) * C : (e - a + 1) * C],
-                    lhsT=w2w[:, e, :].bitcast(FP4X4),
-                    lhsT_scale=w2s[:, e, :],
-                    rhs=codes[:, e * C : (e + 1) * C].bitcast(FP8X4),
-                    rhs_scale=code_scales[:, e * C : (e + 1) * C],
+                    out=res[:, lo - a : hi - a],
+                    lhsT=w2w[:, lo // C, :].bitcast(FP4X4),
+                    lhsT_scale=w2s[:, lo // C, :],
+                    rhs=codes[:, lo:hi].bitcast(FP8X4),
+                    rhs_scale=code_scales[:, lo:hi],
                     start=True,
                     stop=True,
                 )
             if k in EVAC_ON_VECTOR:
-                nc.vector.tensor_copy(y[:, a * C : b * C], res[:, 0 : (b - a) * C])
+                nc.vector.tensor_copy(y[:, a:b], res[:, 0 : b - a])
             else:
-                nc.scalar.copy(y[:, a * C : b * C], res[:, 0 : (b - a) * C])
+                nc.scalar.copy(y[:, a:b], res[:, 0 : b - a])
 
         part = [keep.tile([P, T], F32, name="part%d" % r, align_bytes=64) for r in range(TOP)]
         by_token = keep.tile([P, REST], F32, name="by_token", align_bytes=64)

@@ -23,17 +23,17 @@ ADD = mybir.AluOpType.add
 P = 128
 CH = 128
 BANKS = 8
+BANK_COLUMNS = 512
 STACKED = 8
-W1_GROUPS = ((0, 3), (3, 6), (6, 9))
-FIRST = 128
-EARLY = 640
-BANKFULS = ((0, 512), (512, 1024), (1024, 1536), (1536, 2048), (2048, 2176), (2176, 2304))
-QUANT = ((0, 1024), (1024, 1536), (1536, 2048), (2048, 2176), (2176, 2304))
-EVAC_ON_VECTOR = (2, 3)
-DEALT_ON_VECTOR = ()
-LATE_CUTS = (640, 1024, 1408, 1792, 2048, 2304)
-SUMMED = ((0, 384), (384, 640))
-REST = 640
+W1_GROUP = 3
+
+EARLY_SCALES = 5 * CH
+EARLY_WORDS = 8 * CH
+LATE_CUTS = (EARLY_SCALES, EARLY_WORDS, 11 * CH, 14 * CH, 16 * CH, S)
+QUANTIZE_CUTS = (0, 4 * C, 6 * C, 8 * C, S - CH, S)
+RESULT_CUTS = (0, 2 * C, 4 * C, 6 * C, 8 * C, S - CH, S)
+EMPTIED_BY_VECTOR = (2, 3)
+SUMMED_ON_TENSOR = 512
 
 
 def tile_moe_pkd_mlp_silu_kernel(
@@ -41,7 +41,7 @@ def tile_moe_pkd_mlp_silu_kernel(
 ):
     nc = tc.nc
     with ExitStack() as ctx:
-        held = ctx.enter_context(tc.tile_pool(name="held", bufs=1))
+        shared = ctx.enter_context(tc.tile_pool(name="shared", bufs=1))
         lists = ctx.enter_context(tc.tile_pool(name="lists", bufs=1))
         keep = ctx.enter_context(tc.tile_pool(name="keep", bufs=1))
         psum = ctx.enter_context(tc.psum_pool(name="psum", bufs=1))
@@ -50,12 +50,13 @@ def tile_moe_pkd_mlp_silu_kernel(
         pos_sb = [lists.tile([P, T // 16], U16, name="pos_sb%d" % r) for r in range(TOP)]
         xw = keep.tile([P, T], U32, name="xw", align_bytes=64)
         xs = keep.tile([P, T], U8, name="xs", align_bytes=64)
-        w1w = [keep.tile([P, b - a, 2 * H], U8, name="w1w%d" % a, align_bytes=64) for a, b in W1_GROUPS]
-        s_raw = keep.tile([P, H], U8, name="s_raw", align_bytes=64)
-        s_dealt = held.tile([P, 4, P], U8, name="s_dealt", align_bytes=64, offset=4 * (S - EARLY) - 256)
+        w1w = [keep.tile([P, W1_GROUP, 2 * H], U8, name="w1w%d" % g, align_bytes=64) for g in range(E // W1_GROUP)]
+        late_words_bytes = 4 * (S - EARLY_WORDS)
+        stack_raw = keep.tile([P, H], U8, name="stack_raw", align_bytes=64)
+        stack_dealt = shared.tile([P, 4, P], U8, name="stack_dealt", align_bytes=64, offset=late_words_bytes - H // 2)
         last_raw = keep.tile([P, H], U8, name="last_raw", align_bytes=64)
-        s_last = keep.tile([P, 4, P], U8, name="s_last", align_bytes=64)
-        s_planes = keep.tile([P, STACKED, 4, P], U8, name="s_planes", align_bytes=64)
+        last_plane = keep.tile([P, 4, P], U8, name="last_plane", align_bytes=64)
+        w1_planes = keep.tile([P, STACKED, 4, P], U8, name="w1_planes", align_bytes=64)
         w2w = keep.tile([P, E, 2 * N], U8, name="w2w", align_bytes=64)
         w2s = keep.tile([P, E, N], U8, name="w2s", align_bytes=64)
         gate_sb = keep.tile([P, TOP, T], F32, name="gate_sb", align_bytes=64)
@@ -64,49 +65,50 @@ def tile_moe_pkd_mlp_silu_kernel(
         zero = keep.tile([P, 1], F32, name="zero")
         zero_bias = keep.tile([P, 1], F32, name="zero_bias")
         dealt = [keep.tile([P, 4, 2 * P], U8, name="dealt%d" % e, align_bytes=64) for e in range(E)]
-        bank = [psum.tile([P, 4 * CH], F32, name="bank%d" % b) for b in range(BANKS)]
+        bank = [psum.tile([P, BANK_COLUMNS], F32, name="bank%d" % b) for b in range(BANKS)]
 
-        def load_w1_words(g, queue):
-            a, b = W1_GROUPS[g]
-            queue.dma_start(w1w[g][:].bitcast(I32), w1_words[a:b, 0].rearrange("e p n -> p e n").bitcast(I32))
+        def load_w1_words(g):
+            experts = w1_words[g * W1_GROUP : (g + 1) * W1_GROUP, 0]
+            nc.sync.dma_start(w1w[g][:].bitcast(I32), experts.rearrange("e p n -> p e n").bitcast(I32))
 
-        def load_xs(q, queue):
+        def load_token_scales(q, queue):
             queue.dma_start(xs[32 * q : 32 * q + 4, :].bitcast(I32), x_scales[0, 4 * q : 4 * q + 4, :].bitcast(I32))
 
+        def deal(engine, dst, src):
+            engine.tensor_copy(dst, src.rearrange("p (m t) -> p t m", t=4))
+
         def deal_words(e):
-            for g, (a, b) in enumerate(W1_GROUPS):
-                if a <= e < b:
-                    (nc.vector if e in DEALT_ON_VECTOR else nc.gpsimd).tensor_copy(
-                        dealt[e][:].bitcast(U16), w1w[g][:, e - a, :].bitcast(U16).rearrange("p (m t) -> p t m", t=4)
-                    )
+            deal(nc.gpsimd, dealt[e][:].bitcast(U16), w1w[e // W1_GROUP][:, e % W1_GROUP, :].bitcast(U16))
 
         nc.gpsimd.memset(xs[:].bitcast(I32), 0)
         nc.vector.memset(zero[:], 0.0)
-        nc.vector.memset(s_planes[:].rearrange("p j t m -> p (j t m)").bitcast(I32), 0)
+        nc.vector.memset(w1_planes[:].rearrange("p j t m -> p (j t m)").bitcast(I32), 0)
         nc.vector.memset(w2s[:].bitcast(I32), 0)
         nc.vector.memset(last_raw[:].bitcast(I32), 0)
         make_identity(nc, ident[:])
 
-        nc.scalar.dma_start(s_raw[:].bitcast(I32), w1_scales[0:STACKED, 0].rearrange("e f n -> f e n").bitcast(I32))
+        nc.scalar.dma_start(stack_raw[:].bitcast(I32), w1_scales[0:STACKED, 0].rearrange("e f n -> f e n").bitcast(I32))
         nc.sync.dma_start(offs_sb[:], offs)
-        load_xs(2, nc.scalar)
-        load_xs(0, nc.sync)
-        load_xs(3, nc.scalar)
-        load_xs(1, nc.sync)
+        load_token_scales(2, nc.scalar)
+        load_token_scales(0, nc.sync)
+        load_token_scales(3, nc.scalar)
+        load_token_scales(1, nc.sync)
         nc.sync.dma_start(xw[:].bitcast(I32), x_words[0].rearrange("p t r -> p (t r)").bitcast(I32))
-        load_w1_words(0, nc.sync)
+        load_w1_words(0)
         nc.scalar.activation(zero_bias[:], zero[:], SILU)
 
-        nc.vector.tensor_copy(s_dealt[:], s_raw[:].rearrange("p (m t) -> p t m", t=4))
+        deal(nc.vector, stack_dealt[:], stack_raw[:])
         for q in (0, 2, 1, 3):
             nc.sync.dma_start(
-                s_planes[32 * q : 32 * q + 4].rearrange("p j t m -> p j (t m)").bitcast(I32),
-                s_dealt[32 * q : 32 * q + 32].rearrange("p t m -> p (t m)").bitcast(I32),
+                w1_planes[32 * q : 32 * q + 4].rearrange("p j t m -> p j (t m)").bitcast(I32),
+                stack_dealt[32 * q : 32 * q + 32].rearrange("p t m -> p (t m)").bitcast(I32),
             )
-        load_w1_words(1, nc.sync)
-        load_w1_words(2, nc.sync)
+        load_w1_words(1)
+        load_w1_words(2)
         for q in range(4):
-            nc.sync.dma_start(last_raw[32 * q : 32 * q + 4, :].bitcast(I32), w1_scales[E - 1, 0, 4 * q : 4 * q + 4, :].bitcast(I32))
+            nc.sync.dma_start(
+                last_raw[32 * q : 32 * q + 4, :].bitcast(I32), w1_scales[E - 1, 0, 4 * q : 4 * q + 4, :].bitcast(I32)
+            )
         nc.sync.dma_start(w2w[:].bitcast(I32), w2_words[:, 0].rearrange("e p n -> p e n").bitcast(I32))
         for q in range(4):
             nc.sync.dma_start(
@@ -117,112 +119,114 @@ def tile_moe_pkd_mlp_silu_kernel(
             nc.sync.dma_start(pos_sb[r][:], pos)
         nc.sync.dma_start(gate_sb[:], gate.rearrange("r p t -> p r t"))
 
-        for e in range(E - 1):
+        for e in range(STACKED):
             deal_words(e)
-        nc.gpsimd.tensor_copy(s_last[:], last_raw[:].rearrange("p (m t) -> p t m", t=4))
+        deal(nc.gpsimd, last_plane[:], last_raw[:])
         deal_words(E - 1)
 
-        def w1_plane(e, t):
-            if e == E - 1:
-                return s_last[:, t, :]
-            return s_planes[:, e, t, :]
+        words_first = keep.tile([P, CH], U32, name="words_first", align_bytes=64)
+        words_early = keep.tile([P, EARLY_WORDS - CH], U32, name="words_early", align_bytes=64)
+        scales_first = keep.tile([P, CH], U8, name="scales_first", align_bytes=64)
+        scales_early = keep.tile([P, EARLY_SCALES - CH], U8, name="scales_early", align_bytes=64)
+        hidden = keep.tile([P, S * 4], BF16, name="hidden", align_bytes=64)
 
-        words_first = keep.tile([P, FIRST], U32, name="words_first", align_bytes=64)
-        words_early = keep.tile([P, EARLY - FIRST], U32, name="words_early", align_bytes=64)
-        scales_first = keep.tile([P, FIRST], U8, name="scales_first", align_bytes=64)
-        scales_early = keep.tile([P, EARLY - FIRST], U8, name="scales_early", align_bytes=64)
+        def gather(dst, first_slot, window, lo, hi):
+            nc.vector.tensor_copy(dst[:, lo - first_slot : hi - first_slot], window[:].indirect(offs_sb[:, lo // 16 : hi // 16]))
 
-        def gather(dst, window, a, b):
-            nc.vector.tensor_copy(dst, window[:].indirect(offs_sb[:, a // 16 : b // 16]))
-
-        grouped = keep.tile([P, S * 4], BF16, name="grouped", align_bytes=64)
-
-        def first_layer(c, words, scales):
-            e = c // 2
-            acc = bank[c % BANKS]
+        def first_layer(chunk, words, scales):
+            e = chunk * CH // C
+            acc = bank[chunk % BANKS]
             for t in range(4):
                 nc.tensor.matmul_mx(
                     out=acc[:, t * CH : (t + 1) * CH],
                     lhsT=dealt[e][:, t, :].bitcast(FP4X4),
-                    lhsT_scale=w1_plane(e, t),
+                    lhsT_scale=w1_planes[:, e, t, :] if e < STACKED else last_plane[:, t, :],
                     rhs=words.bitcast(FP8X4),
                     rhs_scale=scales,
                     start=True,
                     stop=True,
                 )
-            dst = grouped[:, c * 4 * CH : (c + 1) * 4 * CH].rearrange("p (s t) -> p s t", t=4)
+            dst = hidden[:, chunk * 4 * CH : (chunk + 1) * 4 * CH].rearrange("p (s t) -> p s t", t=4)
             src = acc[:].rearrange("p (t s) -> p s t", t=4)
-            if c == 0:
+            if chunk == 0:
                 nc.scalar.activation(dst, src, SILU, bias=zero_bias[:])
             else:
                 nc.scalar.activation(dst, src, SILU)
 
-        gather(scales_first[:], xs, 0, FIRST)
-        gather(scales_early[:], xs, FIRST, EARLY)
-        gather(words_first[:], xw, 0, FIRST)
-        gather(words_early[:], xw, FIRST, EARLY)
-        for c in range(FIRST // CH):
-            first_layer(c, words_first[:, c * CH : (c + 1) * CH], scales_first[:, c * CH : (c + 1) * CH])
-        words_late = held.tile([P, S - EARLY], U32, name="words_late", align_bytes=64, offset=0)
-        scales_late = held.tile([P, S - EARLY], U8, name="scales_late", align_bytes=64, offset=4 * (S - EARLY))
-        for a, b in zip(LATE_CUTS, LATE_CUTS[1:]):
-            gather(words_late[:, a - EARLY : b - EARLY], xw, a, b)
-            gather(scales_late[:, a - EARLY : b - EARLY], xs, a, b)
-        for c in range(FIRST // CH, 2 * E):
-            if c < EARLY // CH:
-                cols = slice(c * CH - FIRST, (c + 1) * CH - FIRST)
-                first_layer(c, words_early[:, cols], scales_early[:, cols])
-            else:
-                cols = slice((c - EARLY // CH) * CH, (c - EARLY // CH + 1) * CH)
-                first_layer(c, words_late[:, cols], scales_late[:, cols])
+        gather(scales_first, 0, xs, 0, CH)
+        gather(scales_early, CH, xs, CH, EARLY_SCALES)
+        gather(words_first, 0, xw, 0, CH)
+        gather(words_early, CH, xw, CH, EARLY_SCALES)
+        gather(words_early, CH, xw, EARLY_SCALES, EARLY_WORDS)
+        first_layer(0, words_first[:], scales_first[:])
+        words_late = shared.tile([P, S - EARLY_WORDS], U32, name="words_late", align_bytes=64, offset=0)
+        scales_late = shared.tile([P, S - EARLY_SCALES], U8, name="scales_late", align_bytes=64, offset=late_words_bytes)
+        for lo, hi in zip(LATE_CUTS, LATE_CUTS[1:]):
+            if lo >= EARLY_WORDS:
+                gather(words_late, EARLY_WORDS, xw, lo, hi)
+            gather(scales_late, EARLY_SCALES, xs, lo, hi)
+        chunks = S // CH
+        for chunk in range(1, chunks):
+            lo = chunk * CH
+            words, words_from = (words_early, CH) if lo < EARLY_WORDS else (words_late, EARLY_WORDS)
+            scales, scales_from = (scales_early, CH) if lo < EARLY_SCALES else (scales_late, EARLY_SCALES)
+            first_layer(
+                chunk, words[:, lo - words_from : lo - words_from + CH], scales[:, lo - scales_from : lo - scales_from + CH]
+            )
 
         codes = keep.tile([P, S], U32, name="codes", align_bytes=64)
         code_scales = keep.tile([P, S], U8, name="code_scales", align_bytes=64)
-        for a, b in QUANT:
-            nc.vector.quantize_mx(out=codes[:, a:b].bitcast(FP8X4), scales=code_scales[:, a:b], in_=grouped[:, 4 * a : 4 * b])
-        for k, (a, b) in enumerate(BANKFULS):
-            res = bank[(2 * E - BANKS + k) % BANKS]
-            for lo in range(a, b, C):
-                hi = min(b, lo + C)
+        for lo, hi in zip(QUANTIZE_CUTS, QUANTIZE_CUTS[1:]):
+            nc.vector.quantize_mx(out=codes[:, lo:hi].bitcast(FP8X4), scales=code_scales[:, lo:hi], in_=hidden[:, 4 * lo : 4 * hi])
+        for run, (lo, hi) in enumerate(zip(RESULT_CUTS, RESULT_CUTS[1:])):
+            res = bank[(chunks + run) % BANKS]
+            for start in range(lo, hi, C):
+                stop = min(hi, start + C)
                 nc.tensor.matmul_mx(
-                    out=res[:, lo - a : hi - a],
-                    lhsT=w2w[:, lo // C, :].bitcast(FP4X4),
-                    lhsT_scale=w2s[:, lo // C, :],
-                    rhs=codes[:, lo:hi].bitcast(FP8X4),
-                    rhs_scale=code_scales[:, lo:hi],
+                    out=res[:, start - lo : stop - lo],
+                    lhsT=w2w[:, start // C, :].bitcast(FP4X4),
+                    lhsT_scale=w2s[:, start // C, :],
+                    rhs=codes[:, start:stop].bitcast(FP8X4),
+                    rhs_scale=code_scales[:, start:stop],
                     start=True,
                     stop=True,
                 )
-            if k in EVAC_ON_VECTOR:
-                nc.vector.tensor_copy(y[:, a:b], res[:, 0 : b - a])
+            if run in EMPTIED_BY_VECTOR:
+                nc.vector.tensor_copy(y[:, lo:hi], res[:, 0 : hi - lo])
             else:
-                nc.scalar.copy(y[:, a:b], res[:, 0 : b - a])
+                nc.scalar.copy(y[:, lo:hi], res[:, 0 : hi - lo])
 
-        part = [keep.tile([P, T], F32, name="part%d" % r, align_bytes=64) for r in range(TOP)]
-        by_token = keep.tile([P, REST], F32, name="by_token", align_bytes=64)
-        total = keep.tile([P, REST], F32, name="total", align_bytes=64)
-        for a, b in SUMMED + ((REST, T),):
+        product = [keep.tile([P, T], F32, name="product%d" % r, align_bytes=64) for r in range(TOP)]
+        by_token = keep.tile([P, SUMMED_ON_TENSOR], F32, name="by_token", align_bytes=64)
+        total = keep.tile([P, SUMMED_ON_TENSOR], F32, name="total", align_bytes=64)
+        for lo, hi in ((0, SUMMED_ON_TENSOR), (SUMMED_ON_TENSOR, T)):
             for r in range(TOP):
-                nc.vector.tensor_tensor(part[r][:, a:b], y[:].indirect(pos_sb[r][:, a // 16 : b // 16]), gate_sb[:, r, a:b], MULT)
-        nc.vector.tensor_tensor(part[0][:, REST:T], part[0][:, REST:T], part[1][:, REST:T], ADD)
-        nc.vector.tensor_tensor(part[0][:, REST:T], part[0][:, REST:T], part[2][:, REST:T], ADD)
+                nc.vector.tensor_tensor(
+                    product[r][:, lo:hi], y[:].indirect(pos_sb[r][:, lo // 16 : hi // 16]), gate_sb[:, r, lo:hi], MULT
+                )
+        rest = slice(SUMMED_ON_TENSOR, T)
+        for r in range(1, TOP):
+            nc.vector.tensor_tensor(product[0][:, rest], product[0][:, rest], product[r][:, rest], ADD)
 
-        for k, (a, b) in enumerate(SUMMED):
-            back = bank[REST // P + k]
-            for r in range(TOP):
-                for lo in range(a, b, P):
-                    nc.tensor.matmul(
-                        bank[lo // P][:, 0:P],
-                        part[r][:, lo : lo + P],
-                        ident[:],
-                        start=(r == 0),
-                        stop=(r == TOP - 1),
-                        is_transpose=True,
-                    )
-            for lo in range(a, b, P):
-                nc.scalar.copy(by_token[:, lo : lo + P], bank[lo // P][:, 0:P])
-            for lo in range(a, b, P):
-                nc.tensor.transpose(back[:, lo - a : lo - a + P], by_token[:, lo : lo + P], ident[:])
-            nc.scalar.copy(total[:, a:b], back[:, 0 : b - a])
-            (nc.sync, nc.scalar)[k].dma_start(out[:, a:b], total[:, a:b])
-        nc.sync.dma_start(out[:, REST:T], part[0][:, REST:T])
+        blocks = range(SUMMED_ON_TENSOR // P)
+        for r in range(TOP):
+            for blk in blocks:
+                nc.tensor.matmul(
+                    bank[blk][:, 0:P],
+                    product[r][:, blk * P : (blk + 1) * P],
+                    ident[:],
+                    start=(r == 0),
+                    stop=(r == TOP - 1),
+                    is_transpose=True,
+                )
+        for blk in blocks:
+            nc.scalar.copy(by_token[:, blk * P : (blk + 1) * P], bank[blk][:, 0:P])
+        for pair, queue in enumerate((nc.sync, nc.scalar)):
+            back = bank[len(blocks) + pair]
+            cols = slice(pair * 2 * P, (pair + 1) * 2 * P)
+            for j in range(2):
+                blk = 2 * pair + j
+                nc.tensor.transpose(back[:, j * P : (j + 1) * P], by_token[:, blk * P : (blk + 1) * P], ident[:])
+            nc.scalar.copy(total[:, cols], back[:, 0 : 2 * P])
+            queue.dma_start(out[:, cols], total[:, cols])
+        nc.sync.dma_start(out[:, rest], product[0][:, rest])

@@ -17,6 +17,7 @@ U8 = mybir.dt.uint8
 FP8X4 = mybir.dt.float8_e4m3fn_x4
 FP4X4 = mybir.dt.float4_e2m1fn_x4
 SILU = mybir.ActivationFunctionType.Silu
+COPY = mybir.ActivationFunctionType.Copy
 MULT = mybir.AluOpType.mult
 ADD = mybir.AluOpType.add
 
@@ -33,7 +34,7 @@ LATE_CUTS = (EARLY_SCALES, EARLY_WORDS, 11 * CH, 14 * CH, 16 * CH, S)
 QUANTIZE_CUTS = (0, 4 * C, 6 * C, 8 * C, S - CH, S)
 RESULT_CUTS = (0, 2 * C, 4 * C, 6 * C, 8 * C, S - CH, S)
 EMPTIED_BY_VECTOR = (2, 3)
-SUMMED_ON_TENSOR = 512
+TWICE_ON_SCALAR = 256
 
 
 def tile_moe_pkd_mlp_silu_kernel(
@@ -59,7 +60,9 @@ def tile_moe_pkd_mlp_silu_kernel(
         w1_planes = keep.tile([P, STACKED, 4, P], U8, name="w1_planes", align_bytes=64)
         w2w = keep.tile([P, E, 2 * N], U8, name="w2w", align_bytes=64)
         w2s = keep.tile([P, E, N], U8, name="w2s", align_bytes=64)
-        gate_sb = keep.tile([P, TOP, T], F32, name="gate_sb", align_bytes=64)
+        gate0 = keep.tile([P, T], F32, name="gate0", align_bytes=64)
+        gate1 = keep.tile([P, T - TWICE_ON_SCALAR], F32, name="gate1", align_bytes=64)
+        gate_columns = [keep.tile([P, T // P], F32, name="gate_columns%d" % r, align_bytes=64) for r in (1, 2)]
         y = keep.tile([P, S], F32, name="y", align_bytes=64)
         ident = keep.tile([P, P], F32, name="ident", align_bytes=64)
         zero = keep.tile([P, 1], F32, name="zero")
@@ -117,7 +120,11 @@ def tile_moe_pkd_mlp_silu_kernel(
             )
         for r, pos in enumerate((pos1, pos2, pos3)):
             nc.sync.dma_start(pos_sb[r][:], pos)
-        nc.sync.dma_start(gate_sb[:], gate.rearrange("r p t -> p r t"))
+        nc.sync.dma_start(gate0[:], gate[0])
+        nc.sync.dma_start(gate1[:], gate[1, :, TWICE_ON_SCALAR:T])
+        with nc.allow_non_contiguous_dma(reason="one weight to a partition"):
+            for r in (1, 2):
+                nc.sync.dma_start(gate_columns[r - 1][:], gate[r, 0, :].rearrange("(b p) -> p b", p=P))
 
         for e in range(STACKED):
             deal_words(e)
@@ -196,37 +203,58 @@ def tile_moe_pkd_mlp_silu_kernel(
             else:
                 nc.scalar.copy(y[:, lo:hi], res[:, 0 : hi - lo])
 
-        product = [keep.tile([P, T], F32, name="product%d" % r, align_bytes=64) for r in range(TOP)]
-        by_token = keep.tile([P, SUMMED_ON_TENSOR], F32, name="by_token", align_bytes=64)
-        total = keep.tile([P, SUMMED_ON_TENSOR], F32, name="total", align_bytes=64)
-        for lo, hi in ((0, SUMMED_ON_TENSOR), (SUMMED_ON_TENSOR, T)):
-            for r in range(TOP):
-                nc.vector.tensor_tensor(
-                    product[r][:, lo:hi], y[:].indirect(pos_sb[r][:, lo // 16 : hi // 16]), gate_sb[:, r, lo:hi], MULT
-                )
-        rest = slice(SUMMED_ON_TENSOR, T)
-        for r in range(1, TOP):
-            nc.vector.tensor_tensor(product[0][:, rest], product[0][:, rest], product[r][:, rest], ADD)
+        few = slice(0, TWICE_ON_SCALAR)
+        many = slice(TWICE_ON_SCALAR, T)
 
-        blocks = range(SUMMED_ON_TENSOR // P)
-        for r in range(TOP):
-            for blk in blocks:
+        def fetched(r, cols):
+            return y[:].indirect(pos_sb[r][:, cols.start // 16 : cols.stop // 16])
+
+        product0 = keep.tile([P, T], F32, name="product0", align_bytes=64)
+        product1 = keep.tile([P, T - TWICE_ON_SCALAR], F32, name="product1", align_bytes=64)
+        plain2 = keep.tile([P, T], F32, name="plain2", align_bytes=64)
+        plain1 = keep.tile([P, TWICE_ON_SCALAR], F32, name="plain1", align_bytes=64)
+        turned2 = keep.tile([P, T], F32, name="turned2", align_bytes=64)
+        turned1 = keep.tile([P, TWICE_ON_SCALAR], F32, name="turned1", align_bytes=64)
+        total = keep.tile([P, T], F32, name="total", align_bytes=64)
+
+        nc.vector.tensor_tensor(product1[:], fetched(1, many), gate1[:], MULT)
+        nc.vector.tensor_tensor(product0[:, many], fetched(0, many), gate0[:, many], MULT)
+        nc.vector.tensor_tensor(product0[:, few], fetched(0, few), gate0[:, few], MULT)
+        nc.vector.tensor_tensor(product1[:], product1[:], product0[:, many], ADD)
+        nc.scalar.activation(plain2[:, many], fetched(2, many), COPY)
+        nc.scalar.activation(plain2[:, few], fetched(2, few), COPY)
+        nc.scalar.activation(plain1[:], fetched(1, few), COPY)
+
+        def turn_pair(acc, plain, first_block):
+            for j in range(2):
+                blk = first_block + j
+                nc.tensor.transpose(acc[:, j * P : (j + 1) * P], plain[:, blk * P : (blk + 1) * P], ident[:])
+
+        def weigh_pair(acc, turned, r, first_block):
+            for j in range(2):
+                blk = first_block + j
+                nc.scalar.activation(
+                    turned[:, blk * P : (blk + 1) * P], acc[:, j * P : (j + 1) * P], COPY, scale=gate_columns[r - 1][:, blk : blk + 1]
+                )
+
+        pairs = ((plain2, turned2, 2, 2), (plain2, turned2, 2, 4), (plain2, turned2, 2, 0), (plain1, turned1, 1, 0))
+        for b, (plain, turned, r, first_block) in enumerate(pairs):
+            turn_pair(bank[b], plain, first_block)
+        for b, (plain, turned, r, first_block) in enumerate(pairs):
+            weigh_pair(bank[b], turned, r, first_block)
+        for blk in range(2, 6):
+            nc.tensor.transpose(bank[4][:, (blk - 2) * P : (blk - 1) * P], turned2[:, blk * P : (blk + 1) * P], ident[:])
+        for blk in range(2):
+            for turned in (turned2, turned1):
                 nc.tensor.matmul(
-                    bank[blk][:, 0:P],
-                    product[r][:, blk * P : (blk + 1) * P],
+                    bank[5][:, blk * P : (blk + 1) * P],
+                    turned[:, blk * P : (blk + 1) * P],
                     ident[:],
-                    start=(r == 0),
-                    stop=(r == TOP - 1),
+                    start=(turned is turned2),
+                    stop=(turned is turned1),
                     is_transpose=True,
                 )
-        for blk in blocks:
-            nc.scalar.copy(by_token[:, blk * P : (blk + 1) * P], bank[blk][:, 0:P])
-        for pair, queue in enumerate((nc.sync, nc.scalar)):
-            back = bank[len(blocks) + pair]
-            cols = slice(pair * 2 * P, (pair + 1) * 2 * P)
-            for j in range(2):
-                blk = 2 * pair + j
-                nc.tensor.transpose(back[:, j * P : (j + 1) * P], by_token[:, blk * P : (blk + 1) * P], ident[:])
-            nc.scalar.copy(total[:, cols], back[:, 0 : 2 * P])
-            queue.dma_start(out[:, cols], total[:, cols])
-        nc.sync.dma_start(out[:, rest], product[0][:, rest])
+        nc.vector.tensor_tensor(total[:, many], bank[4][:], product1[:], ADD)
+        nc.sync.dma_start(out[:, many], total[:, many])
+        nc.vector.tensor_tensor(total[:, few], bank[5][:, few], product0[:, few], ADD)
+        nc.sync.dma_start(out[:, few], total[:, few])

@@ -43,6 +43,7 @@ def tile_moe_pkd_mlp_silu_kernel(
     nc = tc.nc
     with ExitStack() as ctx:
         shared = ctx.enter_context(tc.tile_pool(name="shared", bufs=1))
+        reused = ctx.enter_context(tc.tile_pool(name="reused", bufs=1))
         lists = ctx.enter_context(tc.tile_pool(name="lists", bufs=1))
         keep = ctx.enter_context(tc.tile_pool(name="keep", bufs=1))
         psum = ctx.enter_context(tc.psum_pool(name="psum", bufs=1))
@@ -51,12 +52,15 @@ def tile_moe_pkd_mlp_silu_kernel(
         pos_sb = [lists.tile([P, T // 16], U16, name="pos_sb%d" % r) for r in range(TOP)]
         xw = keep.tile([P, T], U32, name="xw", align_bytes=64)
         xs = keep.tile([P, T], U8, name="xs", align_bytes=64)
-        w1w = [keep.tile([P, W1_GROUP, 2 * H], U8, name="w1w%d" % g, align_bytes=64) for g in range(E // W1_GROUP)]
+        w1w = [
+            reused.tile([P, W1_GROUP, 2 * H], U8, name="w1w%d" % g, align_bytes=64, offset=5 * H + g * W1_GROUP * 2 * H)
+            for g in range(E // W1_GROUP)
+        ]
         late_words_bytes = 4 * (S - EARLY_WORDS)
-        stack_raw = keep.tile([P, H], U8, name="stack_raw", align_bytes=64)
+        stack_raw = reused.tile([P, H], U8, name="stack_raw", align_bytes=64, offset=0)
         stack_dealt = shared.tile([P, 4, P], U8, name="stack_dealt", align_bytes=64, offset=late_words_bytes - H // 2)
-        last_raw = keep.tile([P, H], U8, name="last_raw", align_bytes=64)
-        last_plane = keep.tile([P, 4, P], U8, name="last_plane", align_bytes=64)
+        first_raw = reused.tile([P, H], U8, name="first_raw", align_bytes=64, offset=H + 2 * H - H // 2)
+        first_plane = keep.tile([P, 4, P], U8, name="first_plane", align_bytes=64)
         w1_planes = keep.tile([P, STACKED, 4, P], U8, name="w1_planes", align_bytes=64)
         w2w = keep.tile([P, E, 2 * N], U8, name="w2w", align_bytes=64)
         w2s = keep.tile([P, E, N], U8, name="w2s", align_bytes=64)
@@ -64,10 +68,9 @@ def tile_moe_pkd_mlp_silu_kernel(
         gate1 = keep.tile([P, T - TWICE_ON_SCALAR], F32, name="gate1", align_bytes=64)
         gate_columns = [keep.tile([P, T // P], F32, name="gate_columns%d" % r, align_bytes=64) for r in (1, 2)]
         y = keep.tile([P, S], F32, name="y", align_bytes=64)
-        ident = keep.tile([P, P], F32, name="ident", align_bytes=64)
         zero = keep.tile([P, 1], F32, name="zero")
         zero_bias = keep.tile([P, 1], F32, name="zero_bias")
-        dealt = [keep.tile([P, 4, 2 * P], U8, name="dealt%d" % e, align_bytes=64) for e in range(E)]
+        dealt = {}
         bank = [psum.tile([P, BANK_COLUMNS], F32, name="bank%d" % b) for b in range(BANKS)]
 
         def load_w1_words(g):
@@ -77,20 +80,29 @@ def tile_moe_pkd_mlp_silu_kernel(
         def load_token_scales(q, queue):
             queue.dma_start(xs[32 * q : 32 * q + 4, :].bitcast(I32), x_scales[0, 4 * q : 4 * q + 4, :].bitcast(I32))
 
+        def load_first_scales(q, queue):
+            queue.dma_start(first_raw[32 * q : 32 * q + 4, :].bitcast(I32), w1_scales[0, 0, 4 * q : 4 * q + 4, :].bitcast(I32))
+
         def deal(engine, dst, src):
             engine.tensor_copy(dst, src.rearrange("p (m t) -> p t m", t=4))
 
         def deal_words(e):
+            if e in (1, 2):
+                dealt[e] = reused.tile([P, 4, 2 * P], U8, name="dealt%d" % e, align_bytes=64, offset=H + (e - 1) * 2 * H)
+            else:
+                dealt[e] = reused.tile([P, 4, 2 * P], U8, name="dealt%d" % e, align_bytes=64, offset=5 * H + (e - W1_GROUP) * 2 * H)
             deal(nc.gpsimd, dealt[e][:].bitcast(U16), w1w[e // W1_GROUP][:, e % W1_GROUP, :].bitcast(U16))
 
         nc.gpsimd.memset(xs[:].bitcast(I32), 0)
         nc.vector.memset(zero[:], 0.0)
-        nc.vector.memset(w1_planes[:].rearrange("p j t m -> p (j t m)").bitcast(I32), 0)
-        nc.vector.memset(w2s[:].bitcast(I32), 0)
-        nc.vector.memset(last_raw[:].bitcast(I32), 0)
-        make_identity(nc, ident[:])
+        nc.vector.memset(first_raw[:].bitcast(I32), 0)
+        load_first_scales(0, nc.gpsimd)
+        for plane in (w1_planes[:].rearrange("p j t m -> p (j t m)"), w2s[:].rearrange("p e n -> p (e n)")):
+            words = plane.bitcast(I32)
+            nc.vector.memset(words[:, 1:], 0)
+            nc.vector.memset(words[:, 0:1], 0)
 
-        nc.scalar.dma_start(stack_raw[:].bitcast(I32), w1_scales[0:STACKED, 0].rearrange("e f n -> f e n").bitcast(I32))
+        nc.scalar.dma_start(stack_raw[:].bitcast(I32), w1_scales[1:E, 0].rearrange("e f n -> f e n").bitcast(I32))
         nc.sync.dma_start(offs_sb[:], offs)
         load_token_scales(2, nc.scalar)
         load_token_scales(0, nc.sync)
@@ -99,6 +111,8 @@ def tile_moe_pkd_mlp_silu_kernel(
         nc.sync.dma_start(xw[:].bitcast(I32), x_words[0].rearrange("p t r -> p (t r)").bitcast(I32))
         load_w1_words(0)
         nc.scalar.activation(zero_bias[:], zero[:], SILU)
+        for q in (2, 1, 3):
+            load_first_scales(q, nc.scalar)
 
         deal(nc.vector, stack_dealt[:], stack_raw[:])
         for q in (0, 2, 1, 3):
@@ -108,11 +122,6 @@ def tile_moe_pkd_mlp_silu_kernel(
             )
         load_w1_words(1)
         load_w1_words(2)
-        for q in range(4):
-            nc.sync.dma_start(
-                last_raw[32 * q : 32 * q + 4, :].bitcast(I32), w1_scales[E - 1, 0, 4 * q : 4 * q + 4, :].bitcast(I32)
-            )
-        nc.sync.dma_start(w2w[:].bitcast(I32), w2_words[:, 0].rearrange("e p n -> p e n").bitcast(I32))
         for q in range(4):
             nc.sync.dma_start(
                 w2s[32 * q : 32 * q + 4].bitcast(I32),
@@ -125,11 +134,16 @@ def tile_moe_pkd_mlp_silu_kernel(
         with nc.allow_non_contiguous_dma(reason="one weight to a partition"):
             for r in (1, 2):
                 nc.sync.dma_start(gate_columns[r - 1][:], gate[r, 0, :].rearrange("(b p) -> p b", p=P))
+        nc.sync.dma_start(w2w[:].bitcast(I32), w2_words[:, 0].rearrange("e p n -> p e n").bitcast(I32))
 
-        for e in range(STACKED):
+        first_words = keep.tile([P, 4, 2 * P], U8, name="first_words", align_bytes=64)
+        dealt.setdefault(0, first_words)
+        nc.scalar.copy(dealt[0][:].bitcast(U16), w1w[0][:, 0, :].bitcast(U16).rearrange("p (m t) -> p t m", t=4))
+        deal(nc.gpsimd, first_plane[:], first_raw[:])
+        for e in range(1, E):
             deal_words(e)
-        deal(nc.gpsimd, last_plane[:], last_raw[:])
-        deal_words(E - 1)
+        ident = reused.tile([P, P], F32, name="ident", align_bytes=64, offset=0)
+        make_identity(nc, ident[:])
 
         words_first = keep.tile([P, CH], U32, name="words_first", align_bytes=64)
         words_early = keep.tile([P, EARLY_WORDS - CH], U32, name="words_early", align_bytes=64)
@@ -147,7 +161,7 @@ def tile_moe_pkd_mlp_silu_kernel(
                 nc.tensor.matmul_mx(
                     out=acc[:, t * CH : (t + 1) * CH],
                     lhsT=dealt[e][:, t, :].bitcast(FP4X4),
-                    lhsT_scale=w1_planes[:, e, t, :] if e < STACKED else last_plane[:, t, :],
+                    lhsT_scale=w1_planes[:, e - 1, t, :] if e > 0 else first_plane[:, t, :],
                     rhs=words.bitcast(FP8X4),
                     rhs_scale=scales,
                     start=True,
@@ -163,7 +177,8 @@ def tile_moe_pkd_mlp_silu_kernel(
         gather(scales_first, 0, xs, 0, CH)
         gather(scales_early, CH, xs, CH, EARLY_SCALES)
         gather(words_first, 0, xw, 0, CH)
-        gather(words_early, CH, xw, CH, EARLY_SCALES)
+        gather(words_early, CH, xw, CH, C)
+        gather(words_early, CH, xw, C, EARLY_SCALES)
         gather(words_early, CH, xw, EARLY_SCALES, EARLY_WORDS)
         first_layer(0, words_first[:], scales_first[:])
         words_late = shared.tile([P, S - EARLY_WORDS], U32, name="words_late", align_bytes=64, offset=0)

@@ -30,10 +30,11 @@ W1_GROUP = 3
 
 EARLY_SCALES = 5 * CH
 EARLY_WORDS = 8 * CH
-LATE_CUTS = (EARLY_SCALES, EARLY_WORDS, 11 * CH, 14 * CH, 16 * CH, S)
+LATE_SCALE_CUTS = (EARLY_SCALES, EARLY_SCALES + 576, EARLY_SCALES + 2 * 576, S)
+LATE_WORD_CUTS = (EARLY_WORDS, 12 * CH, 16 * CH, S)
 QUANTIZE_CUTS = (0, 4 * C, 6 * C, 8 * C, S - CH, S)
-RESULT_CUTS = (0, 2 * C, 4 * C, 6 * C, 8 * C, S - CH, S)
-EMPTIED_BY_VECTOR = (2, 3)
+RESULT_CUTS = (0, 2 * C, 4 * C, 4 * C + CH, 6 * C, 8 * C, S - CH, S)
+EMPTIED_BY_VECTOR = (3, 4)
 TWICE_ON_SCALAR = 256
 
 
@@ -66,7 +67,8 @@ def tile_moe_pkd_mlp_silu_kernel(
         w2s = keep.tile([P, E, N], U8, name="w2s", align_bytes=64)
         gate0 = keep.tile([P, T], F32, name="gate0", align_bytes=64)
         gate1 = keep.tile([P, T - TWICE_ON_SCALAR], F32, name="gate1", align_bytes=64)
-        gate_columns = [keep.tile([P, T // P], F32, name="gate_columns%d" % r, align_bytes=64) for r in (1, 2)]
+        on_scalar = {1: TWICE_ON_SCALAR, 2: T}
+        gate_columns = {r: keep.tile([P, n // P], F32, name="gate_columns%d" % r, align_bytes=64) for r, n in on_scalar.items()}
         y = keep.tile([P, S], F32, name="y", align_bytes=64)
         zero = keep.tile([P, 1], F32, name="zero")
         zero_bias = keep.tile([P, 1], F32, name="zero_bias")
@@ -133,7 +135,7 @@ def tile_moe_pkd_mlp_silu_kernel(
         nc.sync.dma_start(gate1[:], gate[1, :, TWICE_ON_SCALAR:T])
         with nc.allow_non_contiguous_dma(reason="one weight to a partition"):
             for r in (1, 2):
-                nc.sync.dma_start(gate_columns[r - 1][:], gate[r, 0, :].rearrange("(b p) -> p b", p=P))
+                nc.sync.dma_start(gate_columns[r][:], gate[r, 0, 0 : on_scalar[r]].rearrange("(b p) -> p b", p=P))
         nc.sync.dma_start(w2w[:].bitcast(I32), w2_words[:, 0].rearrange("e p n -> p e n").bitcast(I32))
 
         first_words = keep.tile([P, 4, 2 * P], U8, name="first_words", align_bytes=64)
@@ -177,16 +179,14 @@ def tile_moe_pkd_mlp_silu_kernel(
         gather(scales_first, 0, xs, 0, CH)
         gather(scales_early, CH, xs, CH, EARLY_SCALES)
         gather(words_first, 0, xw, 0, CH)
-        gather(words_early, CH, xw, CH, C)
-        gather(words_early, CH, xw, C, EARLY_SCALES)
+        gather(words_early, CH, xw, CH, EARLY_SCALES)
         gather(words_early, CH, xw, EARLY_SCALES, EARLY_WORDS)
         first_layer(0, words_first[:], scales_first[:])
         words_late = shared.tile([P, S - EARLY_WORDS], U32, name="words_late", align_bytes=64, offset=0)
         scales_late = shared.tile([P, S - EARLY_SCALES], U8, name="scales_late", align_bytes=64, offset=late_words_bytes)
-        for lo, hi in zip(LATE_CUTS, LATE_CUTS[1:]):
-            if lo >= EARLY_WORDS:
-                gather(words_late, EARLY_WORDS, xw, lo, hi)
-            gather(scales_late, EARLY_SCALES, xs, lo, hi)
+        for step in range(3):
+            gather(scales_late, EARLY_SCALES, xs, LATE_SCALE_CUTS[step], LATE_SCALE_CUTS[step + 1])
+            gather(words_late, EARLY_WORDS, xw, LATE_WORD_CUTS[step], LATE_WORD_CUTS[step + 1])
         chunks = S // CH
         for chunk in range(1, chunks):
             lo = chunk * CH
@@ -202,8 +202,8 @@ def tile_moe_pkd_mlp_silu_kernel(
             nc.vector.quantize_mx(out=codes[:, lo:hi].bitcast(FP8X4), scales=code_scales[:, lo:hi], in_=hidden[:, 4 * lo : 4 * hi])
         for run, (lo, hi) in enumerate(zip(RESULT_CUTS, RESULT_CUTS[1:])):
             res = bank[(chunks + run) % BANKS]
-            for start in range(lo, hi, C):
-                stop = min(hi, start + C)
+            starts = [lo] + list(range((lo // C + 1) * C, hi, C))
+            for start, stop in zip(starts, starts[1:] + [hi]):
                 nc.tensor.matmul_mx(
                     out=res[:, start - lo : stop - lo],
                     lhsT=w2w[:, start // C, :].bitcast(FP4X4),
@@ -249,7 +249,7 @@ def tile_moe_pkd_mlp_silu_kernel(
             for j in range(2):
                 blk = first_block + j
                 nc.scalar.activation(
-                    turned[:, blk * P : (blk + 1) * P], acc[:, j * P : (j + 1) * P], COPY, scale=gate_columns[r - 1][:, blk : blk + 1]
+                    turned[:, blk * P : (blk + 1) * P], acc[:, j * P : (j + 1) * P], COPY, scale=gate_columns[r][:, blk : blk + 1]
                 )
 
         pairs = ((plain2, turned2, 2, 2), (plain2, turned2, 2, 4), (plain2, turned2, 2, 0), (plain1, turned1, 1, 0))
@@ -257,19 +257,22 @@ def tile_moe_pkd_mlp_silu_kernel(
             turn_pair(bank[b], plain, first_block)
         for b, (plain, turned, r, first_block) in enumerate(pairs):
             weigh_pair(bank[b], turned, r, first_block)
-        for blk in range(2, 6):
-            nc.tensor.transpose(bank[4][:, (blk - 2) * P : (blk - 1) * P], turned2[:, blk * P : (blk + 1) * P], ident[:])
-        for blk in range(2):
+        many_bank, few_bank = bank[len(pairs)], bank[len(pairs) + 1]
+        few_blocks = TWICE_ON_SCALAR // P
+        for blk in range(few_blocks, T // P):
+            place = blk - few_blocks
+            nc.tensor.transpose(many_bank[:, place * P : (place + 1) * P], turned2[:, blk * P : (blk + 1) * P], ident[:])
+        for blk in range(few_blocks):
             for turned in (turned2, turned1):
                 nc.tensor.matmul(
-                    bank[5][:, blk * P : (blk + 1) * P],
+                    few_bank[:, blk * P : (blk + 1) * P],
                     turned[:, blk * P : (blk + 1) * P],
                     ident[:],
                     start=(turned is turned2),
                     stop=(turned is turned1),
                     is_transpose=True,
                 )
-        nc.vector.tensor_tensor(total[:, many], bank[4][:], product1[:], ADD)
+        nc.vector.tensor_tensor(total[:, many], many_bank[:], product1[:], ADD)
         nc.sync.dma_start(out[:, many], total[:, many])
-        nc.vector.tensor_tensor(total[:, few], bank[5][:, few], product0[:, few], ADD)
+        nc.vector.tensor_tensor(total[:, few], few_bank[:, few], product0[:, few], ADD)
         nc.sync.dma_start(out[:, few], total[:, few])

@@ -80,7 +80,8 @@ def tile_moe_pkd_mlp_silu_kernel(
             nc.sync.dma_start(w1w[g][:].bitcast(I32), experts.rearrange("e p n -> p e n").bitcast(I32))
 
         def load_token_scales(q, queue):
-            queue.dma_start(xs[32 * q : 32 * q + 4, :].bitcast(I32), x_scales[0, 4 * q : 4 * q + 4, :].bitcast(I32))
+            rows = x_scales[0, 4 * q : 4 * q + 4, :].bitcast(I32)
+            queue.dma_start(xs[32 * q : 32 * q + 32, :].bitcast(I32), rows.unsqueeze(0).to_broadcast([8, 4, T // 4]))
 
         def load_first_scales(q, queue):
             queue.dma_start(first_raw[32 * q : 32 * q + 4, :].bitcast(I32), w1_scales[0, 0, 4 * q : 4 * q + 4, :].bitcast(I32))
@@ -95,7 +96,6 @@ def tile_moe_pkd_mlp_silu_kernel(
                 dealt[e] = reused.tile([P, 4, 2 * P], U8, name="dealt%d" % e, align_bytes=64, offset=5 * H + (e - W1_GROUP) * 2 * H)
             deal(nc.gpsimd, dealt[e][:].bitcast(U16), w1w[e // W1_GROUP][:, e % W1_GROUP, :].bitcast(U16))
 
-        nc.gpsimd.memset(xs[:].bitcast(I32), 0)
         nc.vector.memset(zero[:], 0.0)
         nc.vector.memset(first_raw[:].bitcast(I32), 0)
         load_first_scales(0, nc.gpsimd)
@@ -196,7 +196,7 @@ def tile_moe_pkd_mlp_silu_kernel(
                 chunk, words[:, lo - words_from : lo - words_from + CH], scales[:, lo - scales_from : lo - scales_from + CH]
             )
 
-        codes = keep.tile([P, S], U32, name="codes", align_bytes=64)
+        codes = reused.tile([P, S], U32, name="codes", align_bytes=64, offset=5 * H + 2 * W1_GROUP * 2 * H)
         code_scales = keep.tile([P, S], U8, name="code_scales", align_bytes=64)
         for lo, hi in zip(QUANTIZE_CUTS, QUANTIZE_CUTS[1:]):
             nc.vector.quantize_mx(out=codes[:, lo:hi].bitcast(FP8X4), scales=code_scales[:, lo:hi], in_=hidden[:, 4 * lo : 4 * hi])

@@ -86,15 +86,17 @@ def tile_moe_pkd_mlp_silu_kernel(
         def load_first_scales(q, queue):
             queue.dma_start(first_raw[32 * q : 32 * q + 4, :].bitcast(I32), w1_scales[0, 0, 4 * q : 4 * q + 4, :].bitcast(I32))
 
-        def deal(engine, dst, src):
-            engine.tensor_copy(dst, src.rearrange("p (m t) -> p t m", t=4))
+        def deal(engine, dst, src, line):
+            engine.tensor_copy(
+                dst.rearrange("p t (c i) -> p c t i", i=line), src.rearrange("p (c i t) -> p c t i", i=line, t=4)
+            )
 
         def deal_words(e):
             if e in (1, 2):
                 dealt[e] = reused.tile([P, 4, 2 * P], U8, name="dealt%d" % e, align_bytes=64, offset=H + (e - 1) * 2 * H)
             else:
                 dealt[e] = reused.tile([P, 4, 2 * P], U8, name="dealt%d" % e, align_bytes=64, offset=5 * H + (e - W1_GROUP) * 2 * H)
-            deal(nc.gpsimd, dealt[e][:].bitcast(U16), w1w[e // W1_GROUP][:, e % W1_GROUP, :].bitcast(U16))
+            deal(nc.gpsimd, dealt[e][:].bitcast(U16), w1w[e // W1_GROUP][:, e % W1_GROUP, :].bitcast(U16), 8)
 
         nc.vector.memset(zero[:], 0.0)
         nc.vector.memset(first_raw[:].bitcast(I32), 0)
@@ -116,7 +118,7 @@ def tile_moe_pkd_mlp_silu_kernel(
         for q in (2, 1, 3):
             load_first_scales(q, nc.scalar)
 
-        deal(nc.vector, stack_dealt[:], stack_raw[:])
+        deal(nc.vector, stack_dealt[:], stack_raw[:], 16)
         for q in (0, 2, 1, 3):
             nc.sync.dma_start(
                 w1_planes[32 * q : 32 * q + 4].rearrange("p j t m -> p j (t m)").bitcast(I32),
@@ -141,7 +143,7 @@ def tile_moe_pkd_mlp_silu_kernel(
         first_words = keep.tile([P, 4, 2 * P], U8, name="first_words", align_bytes=64)
         dealt.setdefault(0, first_words)
         nc.scalar.copy(dealt[0][:].bitcast(U16), w1w[0][:, 0, :].bitcast(U16).rearrange("p (m t) -> p t m", t=4))
-        deal(nc.gpsimd, first_plane[:], first_raw[:])
+        deal(nc.gpsimd, first_plane[:], first_raw[:], 16)
         for e in range(1, E):
             deal_words(e)
         ident = reused.tile([P, P], F32, name="ident", align_bytes=64, offset=0)

from contextlib import ExitStack

import concourse.mybir as mybir
from concourse.masks import make_identity

K, T, E, C, H, N = 512, 768, 9, 256, 512, 128
TOP = 3
S = E * C
FLOPS = 2 * S * (K * H + H * N)

F32 = mybir.dt.float32
BF16 = mybir.dt.bfloat16
I32 = mybir.dt.int32
U32 = mybir.dt.uint32
U16 = mybir.dt.uint16
U8 = mybir.dt.uint8
FP8X4 = mybir.dt.float8_e4m3fn_x4
FP4X4 = mybir.dt.float4_e2m1fn_x4
SILU = mybir.ActivationFunctionType.Silu
COPY = mybir.ActivationFunctionType.Copy
MULT = mybir.AluOpType.mult
ADD = mybir.AluOpType.add

P = 128
CH = 128
BANKS = 8
BANK_COLUMNS = 512
STACKED = 8
W1_GROUP = 3

EARLY_SCALES = 5 * CH
EARLY_WORDS = 8 * CH
LATE_SCALE_CUTS = (EARLY_SCALES, EARLY_SCALES + 576, EARLY_SCALES + 2 * 576, S)
LATE_WORD_CUTS = (EARLY_WORDS, 12 * CH, 16 * CH, S)
QUANTIZE_CUTS = (0, 4 * C, 6 * C, 8 * C, S - CH, S)
RESULT_CUTS = (0, 2 * C, 4 * C, 4 * C + CH, 6 * C, 8 * C, S - CH, S)
EMPTIED_BY_VECTOR = (3, 4)
TWICE_ON_SCALAR = 256


def tile_moe_pkd_mlp_silu_kernel(
    tc, x_words, x_scales, w1_words, w1_scales, w2_words, w2_scales, gate, offs, pos1, pos2, pos3, out
):
    nc = tc.nc
    with ExitStack() as ctx:
        shared = ctx.enter_context(tc.tile_pool(name="shared", bufs=1))
        reused = ctx.enter_context(tc.tile_pool(name="reused", bufs=1))
        lists = ctx.enter_context(tc.tile_pool(name="lists", bufs=1))
        keep = ctx.enter_context(tc.tile_pool(name="keep", bufs=1))
        psum = ctx.enter_context(tc.psum_pool(name="psum", bufs=1))

        offs_sb = lists.tile([P, S // 16], U16, name="offs_sb")
        pos_sb = [lists.tile([P, T // 16], U16, name="pos_sb%d" % r) for r in range(TOP)]
        xw = keep.tile([P, T], U32, name="xw", align_bytes=64)
        xs = keep.tile([P, T], U8, name="xs", align_bytes=64)
        w1w = [
            reused.tile([P, W1_GROUP, 2 * H], U8, name="w1w%d" % g, align_bytes=64, offset=5 * H + g * W1_GROUP * 2 * H)
            for g in range(E // W1_GROUP)
        ]
        late_words_bytes = 4 * (S - EARLY_WORDS)
        stack_raw = reused.tile([P, H], U8, name="stack_raw", align_bytes=64, offset=0)
        stack_dealt = shared.tile([P, 4, P], U8, name="stack_dealt", align_bytes=64, offset=late_words_bytes - H // 2)
        first_raw = reused.tile([P, H], U8, name="first_raw", align_bytes=64, offset=H + 2 * H - H // 2)
        first_plane = keep.tile([P, 4, P], U8, name="first_plane", align_bytes=64)
        w1_planes = keep.tile([P, STACKED, 4, P], U8, name="w1_planes", align_bytes=64)
        w2w = keep.tile([P, E, 2 * N], U8, name="w2w", align_bytes=64)
        w2s = keep.tile([P, E, N], U8, name="w2s", align_bytes=64)
        gate0 = keep.tile([P, T], F32, name="gate0", align_bytes=64)
        gate1 = keep.tile([P, T - TWICE_ON_SCALAR], F32, name="gate1", align_bytes=64)
        on_scalar = {1: TWICE_ON_SCALAR, 2: T}
        gate_columns = {r: keep.tile([P, n // P], F32, name="gate_columns%d" % r, align_bytes=64) for r, n in on_scalar.items()}
        y = keep.tile([P, S], F32, name="y", align_bytes=64)
        zero = keep.tile([P, 1], F32, name="zero")
        zero_bias = keep.tile([P, 1], F32, name="zero_bias")
        dealt = {}
        bank = [psum.tile([P, BANK_COLUMNS], F32, name="bank%d" % b) for b in range(BANKS)]

        def load_w1_words(g):
            experts = w1_words[g * W1_GROUP : (g + 1) * W1_GROUP, 0]
            nc.sync.dma_start(w1w[g][:].bitcast(I32), experts.rearrange("e p n -> p e n").bitcast(I32))

        def load_token_scales(q, queue):
            rows = x_scales[0, 4 * q : 4 * q + 4, :].bitcast(I32)
            queue.dma_start(xs[32 * q : 32 * q + 32, :].bitcast(I32), rows.unsqueeze(0).to_broadcast([8, 4, T // 4]))

        def load_first_scales(q, queue):
            queue.dma_start(first_raw[32 * q : 32 * q + 4, :].bitcast(I32), w1_scales[0, 0, 4 * q : 4 * q + 4, :].bitcast(I32))

        def deal(engine, dst, src, line):
            engine.tensor_copy(
                dst.rearrange("p t (c i) -> p c t i", i=line), src.rearrange("p (c i t) -> p c t i", i=line, t=4)
            )

        def deal_words(e):
            if e in (1, 2):
                dealt[e] = reused.tile([P, 4, 2 * P], U8, name="dealt%d" % e, align_bytes=64, offset=H + (e - 1) * 2 * H)
            else:
                dealt[e] = reused.tile([P, 4, 2 * P], U8, name="dealt%d" % e, align_bytes=64, offset=5 * H + (e - W1_GROUP) * 2 * H)
            deal(nc.gpsimd, dealt[e][:].bitcast(U16), w1w[e // W1_GROUP][:, e % W1_GROUP, :].bitcast(U16), 8)

        nc.vector.memset(zero[:], 0.0)
        nc.vector.memset(first_raw[:].bitcast(I32), 0)
        load_first_scales(0, nc.gpsimd)
        for plane in (w1_planes[:].rearrange("p j t m -> p (j t m)"), w2s[:].rearrange("p e n -> p (e n)")):
            words = plane.bitcast(I32)
            nc.vector.memset(words[:, 1:], 0)
            nc.vector.memset(words[:, 0:1], 0)

        nc.scalar.dma_start(stack_raw[:].bitcast(I32), w1_scales[1:E, 0].rearrange("e f n -> f e n").bitcast(I32))
        nc.sync.dma_start(offs_sb[:], offs)
        load_token_scales(2, nc.scalar)
        load_token_scales(0, nc.sync)
        load_token_scales(3, nc.scalar)
        load_token_scales(1, nc.sync)
        nc.sync.dma_start(xw[:].bitcast(I32), x_words[0].rearrange("p t r -> p (t r)").bitcast(I32))
        load_w1_words(0)
        nc.scalar.activation(zero_bias[:], zero[:], SILU)
        for q in (2, 1, 3):
            load_first_scales(q, nc.scalar)

        deal(nc.vector, stack_dealt[:], stack_raw[:], 16)
        for q in (0, 2, 1, 3):
            nc.sync.dma_start(
                w1_planes[32 * q : 32 * q + 4].rearrange("p j t m -> p j (t m)").bitcast(I32),
                stack_dealt[32 * q : 32 * q + 32].rearrange("p t m -> p (t m)").bitcast(I32),
            )
        load_w1_words(1)
        load_w1_words(2)
        for q in range(4):
            nc.sync.dma_start(
                w2s[32 * q : 32 * q + 4].bitcast(I32),
                w2_scales[:, 0, 4 * q : 4 * q + 4, :].rearrange("e r n -> r e n").bitcast(I32),
            )
        for r, pos in enumerate((pos1, pos2, pos3)):
            nc.sync.dma_start(pos_sb[r][:], pos)
        nc.sync.dma_start(gate0[:], gate[0])
        nc.sync.dma_start(gate1[:], gate[1, :, TWICE_ON_SCALAR:T])
        with nc.allow_non_contiguous_dma(reason="one weight to a partition"):
            for r in (1, 2):
                nc.sync.dma_start(gate_columns[r][:], gate[r, 0, 0 : on_scalar[r]].rearrange("(b p) -> p b", p=P))
        nc.sync.dma_start(w2w[:].bitcast(I32), w2_words[:, 0].rearrange("e p n -> p e n").bitcast(I32))

        first_words = keep.tile([P, 4, 2 * P], U8, name="first_words", align_bytes=64)
        dealt.setdefault(0, first_words)
        nc.scalar.copy(dealt[0][:].bitcast(U16), w1w[0][:, 0, :].bitcast(U16).rearrange("p (m t) -> p t m", t=4))
        deal(nc.gpsimd, first_plane[:], first_raw[:], 16)
        for e in range(1, E):
            deal_words(e)
        ident = reused.tile([P, P], F32, name="ident", align_bytes=64, offset=0)
        make_identity(nc, ident[:])

        words_first = keep.tile([P, CH], U32, name="words_first", align_bytes=64)
        words_early = keep.tile([P, EARLY_WORDS - CH], U32, name="words_early", align_bytes=64)
        scales_first = keep.tile([P, CH], U8, name="scales_first", align_bytes=64)
        scales_early = keep.tile([P, EARLY_SCALES - CH], U8, name="scales_early", align_bytes=64)
        hidden = keep.tile([P, S * 4], BF16, name="hidden", align_bytes=64)

        def gather(dst, first_slot, window, lo, hi):
            nc.vector.tensor_copy(dst[:, lo - first_slot : hi - first_slot], window[:].indirect(offs_sb[:, lo // 16 : hi // 16]))

        def first_layer(chunk, words, scales):
            e = chunk * CH // C
            acc = bank[chunk % BANKS]
            for t in range(4):
                nc.tensor.matmul_mx(
                    out=acc[:, t * CH : (t + 1) * CH],
                    lhsT=dealt[e][:, t, :].bitcast(FP4X4),
                    lhsT_scale=w1_planes[:, e - 1, t, :] if e > 0 else first_plane[:, t, :],
                    rhs=words.bitcast(FP8X4),
                    rhs_scale=scales,
                    start=True,
                    stop=True,
                )
            dst = hidden[:, chunk * 4 * CH : (chunk + 1) * 4 * CH].rearrange("p (s t) -> p s t", t=4)
            src = acc[:].rearrange("p (t s) -> p s t", t=4)
            if chunk == 0:
                nc.scalar.activation(dst, src, SILU, bias=zero_bias[:])
            else:
                nc.scalar.activation(dst, src, SILU)

        gather(scales_first, 0, xs, 0, CH)
        gather(scales_early, CH, xs, CH, EARLY_SCALES)
        gather(words_first, 0, xw, 0, CH)
        gather(words_early, CH, xw, CH, EARLY_SCALES)
        gather(words_early, CH, xw, EARLY_SCALES, EARLY_WORDS)
        first_layer(0, words_first[:], scales_first[:])
        words_late = shared.tile([P, S - EARLY_WORDS], U32, name="words_late", align_bytes=64, offset=0)
        scales_late = shared.tile([P, S - EARLY_SCALES], U8, name="scales_late", align_bytes=64, offset=late_words_bytes)
        for step in range(3):
            gather(scales_late, EARLY_SCALES, xs, LATE_SCALE_CUTS[step], LATE_SCALE_CUTS[step + 1])
            gather(words_late, EARLY_WORDS, xw, LATE_WORD_CUTS[step], LATE_WORD_CUTS[step + 1])
        chunks = S // CH
        for chunk in range(1, chunks):
            lo = chunk * CH
            words, words_from = (words_early, CH) if lo < EARLY_WORDS else (words_late, EARLY_WORDS)
            scales, scales_from = (scales_early, CH) if lo < EARLY_SCALES else (scales_late, EARLY_SCALES)
            first_layer(
                chunk, words[:, lo - words_from : lo - words_from + CH], scales[:, lo - scales_from : lo - scales_from + CH]
            )

        codes = reused.tile([P, S], U32, name="codes", align_bytes=64, offset=5 * H + 2 * W1_GROUP * 2 * H)
        code_scales = keep.tile([P, S], U8, name="code_scales", align_bytes=64)
        for lo, hi in zip(QUANTIZE_CUTS, QUANTIZE_CUTS[1:]):
            nc.vector.quantize_mx(out=codes[:, lo:hi].bitcast(FP8X4), scales=code_scales[:, lo:hi], in_=hidden[:, 4 * lo : 4 * hi])
        for run, (lo, hi) in enumerate(zip(RESULT_CUTS, RESULT_CUTS[1:])):
            res = bank[(chunks + run) % BANKS]
            starts = [lo] + list(range((lo // C + 1) * C, hi, C))
            for start, stop in zip(starts, starts[1:] + [hi]):
                nc.tensor.matmul_mx(
                    out=res[:, start - lo : stop - lo],
                    lhsT=w2w[:, start // C, :].bitcast(FP4X4),
                    lhsT_scale=w2s[:, start // C, :],
                    rhs=codes[:, start:stop].bitcast(FP8X4),
                    rhs_scale=code_scales[:, start:stop],
                    start=True,
                    stop=True,
                )
            if run in EMPTIED_BY_VECTOR:
                nc.vector.tensor_copy(y[:, lo:hi], res[:, 0 : hi - lo])
            else:
                nc.scalar.copy(y[:, lo:hi], res[:, 0 : hi - lo])

        few = slice(0, TWICE_ON_SCALAR)
        many = slice(TWICE_ON_SCALAR, T)

        def fetched(r, cols):
            return y[:].indirect(pos_sb[r][:, cols.start // 16 : cols.stop // 16])

        product0 = keep.tile([P, T], F32, name="product0", align_bytes=64)
        product1 = keep.tile([P, T - TWICE_ON_SCALAR], F32, name="product1", align_bytes=64)
        plain2 = keep.tile([P, T], F32, name="plain2", align_bytes=64)
        plain1 = keep.tile([P, TWICE_ON_SCALAR], F32, name="plain1", align_bytes=64)
        turned2 = keep.tile([P, T], F32, name="turned2", align_bytes=64)
        turned1 = keep.tile([P, TWICE_ON_SCALAR], F32, name="turned1", align_bytes=64)
        total = keep.tile([P, T], F32, name="total", align_bytes=64)

        nc.vector.tensor_tensor(product1[:], fetched(1, many), gate1[:], MULT)
        nc.vector.tensor_tensor(product0[:, many], fetched(0, many), gate0[:, many], MULT)
        nc.vector.tensor_tensor(product0[:, few], fetched(0, few), gate0[:, few], MULT)
        nc.vector.tensor_tensor(product1[:], product1[:], product0[:, many], ADD)
        nc.scalar.activation(plain2[:, many], fetched(2, many), COPY)
        nc.scalar.activation(plain2[:, few], fetched(2, few), COPY)
        nc.scalar.activation(plain1[:], fetched(1, few), COPY)

        def turn_pair(acc, plain, first_block):
            for j in range(2):
                blk = first_block + j
                nc.tensor.transpose(acc[:, j * P : (j + 1) * P], plain[:, blk * P : (blk + 1) * P], ident[:])

        def weigh_pair(acc, turned, r, first_block):
            for j in range(2):
                blk = first_block + j
                nc.scalar.activation(
                    turned[:, blk * P : (blk + 1) * P], acc[:, j * P : (j + 1) * P], COPY, scale=gate_columns[r][:, blk : blk + 1]
                )

        pairs = ((plain2, turned2, 2, 2), (plain2, turned2, 2, 4), (plain2, turned2, 2, 0), (plain1, turned1, 1, 0))
        for b, (plain, turned, r, first_block) in enumerate(pairs):
            turn_pair(bank[b], plain, first_block)
        for b, (plain, turned, r, first_block) in enumerate(pairs):
            weigh_pair(bank[b], turned, r, first_block)
        many_bank, few_bank = bank[len(pairs)], bank[len(pairs) + 1]
        few_blocks = TWICE_ON_SCALAR // P
        for blk in range(few_blocks, T // P):
            place = blk - few_blocks
            nc.tensor.transpose(many_bank[:, place * P : (place + 1) * P], turned2[:, blk * P : (blk + 1) * P], ident[:])
        for blk in range(few_blocks):
            for turned in (turned2, turned1):
                nc.tensor.matmul(
                    few_bank[:, blk * P : (blk + 1) * P],
                    turned[:, blk * P : (blk + 1) * P],
                    ident[:],
                    start=(turned is turned2),
                    stop=(turned is turned1),
                    is_transpose=True,
                )
        nc.vector.tensor_tensor(total[:, many], many_bank[:], product1[:], ADD)
        nc.sync.dma_start(out[:, many], total[:, many])
        nc.vector.tensor_tensor(total[:, few], few_bank[:, few], product0[:, few], ADD)
        nc.sync.dma_start(out[:, few], total[:, few])
